import numpy as np
import ml_dtypes


def mxq(x, axis, fmt="e4m3"):
    dtype, down = {"e4m3": (ml_dtypes.float8_e4m3fn, 7), "e5m2": (ml_dtypes.float8_e5m2, 14)}[fmt]
    v = np.moveaxis(np.asarray(x, np.float32).astype(ml_dtypes.bfloat16).astype(np.float64), axis, -1)
    blocks = v.reshape(v.shape[:-1] + (-1, 32))
    amax = np.abs(blocks).max(-1, keepdims=True)
    byte = np.maximum(np.where(amax > 0, np.frexp(amax)[1] - 1 + 127, 0) - down, 1)
    scale = np.exp2(byte - 127.0)
    codes = (blocks / scale).astype(np.float32).astype(dtype).astype(np.float64)
    return np.moveaxis((codes * scale).reshape(v.shape), -1, axis)


WIDE = False


def mx_kscale(k):
    if not WIDE:
        return np.ones(k)
    levels = np.array([10, -10, 5, -5, 0])
    if k % 512:
        return np.exp2(np.random.permutation(np.resize(levels, k // 32))).repeat(32)
    a = np.empty((k // 512, 16))
    for p in range(k // 512):
        a[p, :8] = np.random.permutation(np.resize(levels, 8))
        for g in range(8):
            far = levels[np.abs(levels - a[p, g]) >= 10]
            a[p, g + 8] = far[np.random.randint(len(far))]
    return np.exp2(a.ravel()).repeat(32)


def f64(x):
    return np.asarray(x).astype(np.float64)


def striped(idx):
    return np.tile(idx.reshape(-1, 16).T, (8, 1)).astype(np.uint16)


def unstriped(offs):
    return offs[:16].T.reshape(-1).astype(np.int64)


def pack_weight(w):
    k, n = w.shape
    w = f64(np.asarray(w, np.float32).astype(ml_dtypes.bfloat16)).reshape(k // 32, 32, n)
    amax = np.abs(w).max(1)
    byte = np.clip(np.where(amax > 0, np.frexp(amax)[1] - 1 + 127 - 7, 1), 1, 254)
    scaled = (w * np.exp2(127.0 - byte)[:, None, :]).reshape(k, n).astype(np.float32)
    words = np.ascontiguousarray(scaled.reshape(k // 512, 128, 4, n).transpose(0, 1, 3, 2)).astype(ml_dtypes.float8_e4m3fn).view(np.uint8)
    return words, np.ascontiguousarray(byte.astype(np.uint8).reshape(k // 512, 16, n))


def unpack_weight(words, scales):
    g, p, n, _ = words.shape
    vals = np.ascontiguousarray(words).view(ml_dtypes.float8_e4m3fn).astype(np.float64) * np.repeat(np.exp2(scales.astype(np.float64) - 127.0), 8, axis=1)[..., None]
    return vals.transpose(0, 1, 3, 2).reshape(g * 512, n)


K, T, S, N, U = 1024, 1024, 512, 256, 1024


def setup_inputs():
    n = np.random.standard_normal
    s = mx_kscale(K)[:, None]
    packed_w1 = pack_weight(n((K, N)) / np.sqrt(K) / s)
    return {
        "xT": (n((K, T)) * s).astype(np.float32),
        "mem": n((N, U)).astype(np.float32),
        "w1_words": packed_w1[0],
        "w1_scales": packed_w1[1],
        "offs": striped(np.random.permutation(T)[:S]),
        "slot": striped(np.random.permutation(U)[:S]),
    }


def reference(xT, mem, w1_words, w1_scales, offs, slot):
    xq = mxq(f64(xT)[:, unstriped(offs)], 0, "e4m3")
    y = unpack_weight(w1_words, w1_scales).T @ xq
    out = f64(mem).copy()
    out[:, unstriped(slot)] = y
    return out

@@ -1,0 +1,118 @@
+from contextlib import ExitStack
+
+import concourse.mybir as mybir
+
+K, T, S, N, U = 1024, 1024, 512, 256, 1024
+FLOPS = 2 * K * S * N
+
+F32 = mybir.dt.float32
+BF16 = mybir.dt.bfloat16
+I32 = mybir.dt.int32
+U32 = mybir.dt.uint32
+U16 = mybir.dt.uint16
+U8 = mybir.dt.uint8
+FP8X4 = mybir.dt.float8_e4m3fn_x4
+
+P = 128
+PACK = 4
+K_PASS = P * PACK
+PASSES = K // K_PASS
+BLOCKS = N // P
+LIST_ROWS = 16
+PIECES = ((0, 128), (128, 256), (256, 512))
+
+
+def weave(nc, woven, planes):
+    nc.scalar.copy(
+        woven.rearrange("p (c i) t -> p c t i", i=4),
+        planes.rearrange("p t (c i) -> p c t i", i=4),
+    )
+
+
+def tile_picked_kvput_none_e_kernel(tc, xT, mem, w1_words, w1_scales, offs, slot, out):
+    nc = tc.nc
+    with ExitStack() as ctx:
+        keep = ctx.enter_context(tc.tile_pool(name="keep", bufs=1))
+        psum = ctx.enter_context(tc.psum_pool(name="psum", bufs=1))
+
+        offs_sb = keep.tile([P, S // LIST_ROWS], U16, name="offs_sb")
+        slot_sb = keep.tile([P, S // LIST_ROWS], U16, name="slot_sb")
+        w_words = keep.tile([P, PASSES, N], U32, name="w_words", align_bytes=64)
+        w_scales = keep.tile([P, PASSES, N], U8, name="w_scales", align_bytes=64)
+        nc.vector.memset(w_scales[:].bitcast(I32), 0)
+
+        x_rows = xT.rearrange("(z p t) c -> z t p c", z=PASSES, t=PACK)
+        planes = {}
+        for z in range(PASSES):
+            for t in range(PACK):
+                planes[z, t] = keep.tile([P, T], F32, name="plane_%d_%d" % (z, t))
+                nc.sync.dma_start(planes[z, t][:], x_rows[z, t])
+                if (z, t) == (0, 0):
+                    nc.sync.dma_start(offs_sb[:], offs)
+        nc.sync.dma_start(
+            w_words[:].bitcast(I32),
+            w1_words.rearrange("z p n r -> p z (n r)").bitcast(I32),
+        )
+        scale_rows = w1_scales.bitcast(I32).rearrange("z (q i) c -> i q z c", i=4)
+        for i in range(4):
+            nc.sync.dma_start(w_scales[:].bitcast(I32)[i:P:32], scale_rows[i])
+        nc.sync.dma_start(slot_sb[:], slot)
+        windows = []
+        for m in range(BLOCKS):
+            window = keep.tile([P, U], F32, name="window_%d" % m)
+            nc.sync.dma_start(window[:], mem[m * P : (m + 1) * P, :])
+            windows.append(window)
+
+        picked = [keep.tile([P, PACK, S], F32, name="picked_%d" % z) for z in range(PASSES)]
+        woven, codes, scales = {}, {}, {}
+        for z in range(PASSES):
+            for h, (a, b) in enumerate(PIECES):
+                woven[z, h] = keep.tile([P, b - a, PACK], BF16, name="woven_%d_%d" % (z, h), align_bytes=64)
+                codes[z, h] = keep.tile([P, b - a], U32, name="codes_%d_%d" % (z, h), align_bytes=64)
+                scales[z, h] = keep.tile([P, b - a], U8, name="scales_%d_%d" % (z, h), align_bytes=64)
+
+        def quantise(z, h):
+            nc.vector.quantize_mx(
+                out=codes[z, h][:].bitcast(FP8X4),
+                scales=scales[z, h][:],
+                in_=woven[z, h][:].rearrange("p c t -> p (c t)"),
+            )
+
+        for z in range(PASSES):
+            for t in range(PACK):
+                if (z, t) == (PASSES - 1, PACK - 1):
+                    for a, b in PIECES:
+                        nc.vector.tensor_copy(
+                            picked[z][:, t, a:b],
+                            planes[z, t][:].indirect(offs_sb[:, a // LIST_ROWS : b // LIST_ROWS]),
+                        )
+                else:
+                    nc.vector.tensor_copy(picked[z][:, t, :], planes[z, t][:].indirect(offs_sb[:]))
+            for h, (a, b) in enumerate(PIECES):
+                weave(nc, woven[z, h][:], picked[z][:, :, a:b])
+            if z < PASSES - 1:
+                for h in range(len(PIECES)):
+                    quantise(z, h)
+
+        for h, (a, b) in enumerate(PIECES):
+            quantise(PASSES - 1, h)
+            for m in range(BLOCKS):
+                acc = psum.tile([P, b - a], F32, name="acc_%d_%d" % (h, m))
+                for z in range(PASSES):
+                    nc.tensor.matmul_mx(
+                        out=acc[:],
+                        lhsT=w_words[:, z, m * P : (m + 1) * P].bitcast(FP8X4),
+                        lhsT_scale=w_scales[:, z, m * P : (m + 1) * P],
+                        rhs=codes[z, h][:].bitcast(FP8X4),
+                        rhs_scale=scales[z, h][:],
+                        start=(z == 0),
+                        stop=(z == PASSES - 1),
+                    )
+                y = keep.tile([P, b - a], F32, name="y_%d_%d" % (h, m))
+                nc.scalar.copy(y[:], acc[:])
+                nc.vector.tensor_copy(
+                    windows[m][:].indirect(slot_sb[:, a // LIST_ROWS : b // LIST_ROWS]), y[:]
+                )
+
+        for m in range(BLOCKS):
+            nc.sync.dma_start(out[m * P : (m + 1) * P, :], windows[m][:])

@@ -19,14 +19,8 @@ K_PASS = P * PACK
 PASSES = K // K_PASS
 BLOCKS = N // P
 LIST_ROWS = 16
-PIECES = ((0, 128), (128, 256), (256, 512))
-
-
-def weave(nc, woven, planes):
-    nc.scalar.copy(
-        woven.rearrange("p (c i) t -> p c t i", i=4),
-        planes.rearrange("p t (c i) -> p c t i", i=4),
-    )
+PIECE = 128
+PIECES = S // PIECE
 
 
 def tile_picked_kvput_none_e_kernel(tc, xT, mem, w1_words, w1_scales, offs, slot, out):
@@ -63,56 +57,66 @@ def tile_picked_kvput_none_e_kernel(tc, xT, mem, w1_words, w1_scales, offs, slot
             nc.sync.dma_start(window[:], mem[m * P : (m + 1) * P, :])
             windows.append(window)
 
-        picked = [keep.tile([P, PACK, S], F32, name="picked_%d" % z) for z in range(PASSES)]
-        woven, codes, scales = {}, {}, {}
-        for z in range(PASSES):
-            for h, (a, b) in enumerate(PIECES):
-                woven[z, h] = keep.tile([P, b - a, PACK], BF16, name="woven_%d_%d" % (z, h), align_bytes=64)
-                codes[z, h] = keep.tile([P, b - a], U32, name="codes_%d_%d" % (z, h), align_bytes=64)
-                scales[z, h] = keep.tile([P, b - a], U8, name="scales_%d_%d" % (z, h), align_bytes=64)
+        def entries(tile, a, b):
+            return tile[:, a // LIST_ROWS : b // LIST_ROWS]
 
-        def quantise(z, h):
-            nc.vector.quantize_mx(
-                out=codes[z, h][:].bitcast(FP8X4),
-                scales=scales[z, h][:],
-                in_=woven[z, h][:].rearrange("p c t -> p (c t)"),
+        woven = keep.tile([P, PIECES, PASSES, PIECE, PACK], BF16, name="woven", align_bytes=64)
+        pieces = [slice(h * PIECE, (h + 1) * PIECE) for h in range(PIECES)]
+
+        for z, u in ((0, 0), (0, 1), (1, 0)):
+            pair = keep.tile([P, 2, S], F32, name="pair_%d_%d" % (z, u))
+            for e in range(2):
+                nc.vector.tensor_copy(pair[:, e, :], planes[z, 2 * u + e][:].indirect(offs_sb[:]))
+            nc.scalar.copy(
+                woven[:, :, z, :, 2 * u : 2 * u + 2],
+                pair[:].rearrange("p e (h c) -> p h c e", h=PIECES),
             )
 
-        for z in range(PASSES):
-            for t in range(PACK):
-                if (z, t) == (PASSES - 1, PACK - 1):
-                    for a, b in PIECES:
-                        nc.vector.tensor_copy(
-                            picked[z][:, t, a:b],
-                            planes[z, t][:].indirect(offs_sb[:, a // LIST_ROWS : b // LIST_ROWS]),
-                        )
-                else:
-                    nc.vector.tensor_copy(picked[z][:, t, :], planes[z, t][:].indirect(offs_sb[:]))
-            for h, (a, b) in enumerate(PIECES):
-                weave(nc, woven[z, h][:], picked[z][:, :, a:b])
-            if z < PASSES - 1:
-                for h in range(len(PIECES)):
-                    quantise(z, h)
+        last = keep.tile([P, 2, S], F32, name="last")
+        nc.vector.tensor_copy(last[:, 0, :], planes[1, 2][:].indirect(offs_sb[:]))
+        for h in range(PIECES):
+            nc.vector.tensor_copy(
+                last[:, 1, pieces[h]],
+                planes[1, 3][:].indirect(entries(offs_sb, h * PIECE, (h + 1) * PIECE)),
+            )
+        for h in range(PIECES):
+            nc.scalar.copy(woven[:, h, 1, :, 2:4], last[:, :, pieces[h]].rearrange("p e c -> p c e"))
 
-        for h, (a, b) in enumerate(PIECES):
-            quantise(PASSES - 1, h)
-            for m in range(BLOCKS):
-                acc = psum.tile([P, b - a], F32, name="acc_%d_%d" % (h, m))
-                for z in range(PASSES):
-                    nc.tensor.matmul_mx(
-                        out=acc[:],
-                        lhsT=w_words[:, z, m * P : (m + 1) * P].bitcast(FP8X4),
-                        lhsT_scale=w_scales[:, z, m * P : (m + 1) * P],
-                        rhs=codes[z, h][:].bitcast(FP8X4),
-                        rhs_scale=scales[z, h][:],
-                        start=(z == 0),
-                        stop=(z == PASSES - 1),
-                    )
-                y = keep.tile([P, b - a], F32, name="y_%d_%d" % (h, m))
-                nc.scalar.copy(y[:], acc[:])
-                nc.vector.tensor_copy(
-                    windows[m][:].indirect(slot_sb[:, a // LIST_ROWS : b // LIST_ROWS]), y[:]
+        codes = keep.tile([P, PIECES, PASSES, PIECE], U32, name="codes", align_bytes=64)
+        scales = keep.tile([P, PIECES, PASSES, PIECE], U8, name="scales", align_bytes=64)
+
+        def product(acc, m, h):
+            for z in range(PASSES):
+                nc.tensor.matmul_mx(
+                    out=acc,
+                    lhsT=w_words[:, z, m * P : (m + 1) * P].bitcast(FP8X4),
+                    lhsT_scale=w_scales[:, z, m * P : (m + 1) * P],
+                    rhs=codes[:, h, z, :].bitcast(FP8X4),
+                    rhs_scale=scales[:, h, z, :],
+                    start=(z == 0),
+                    stop=(z == PASSES - 1),
                 )
 
-        for m in range(BLOCKS):
-            nc.sync.dma_start(out[m * P : (m + 1) * P, :], windows[m][:])
+        y_first = keep.tile([P, PIECE], F32, name="y_first")
+        y_rest = keep.tile([P, S - PIECE], F32, name="y_rest")
+        for h in range(PIECES):
+            nc.vector.quantize_mx(
+                out=codes[:, h].rearrange("p z c -> p (z c)").bitcast(FP8X4),
+                scales=scales[:, h].rearrange("p z c -> p (z c)"),
+                in_=woven[:, h].rearrange("p z c t -> p (z c t)"),
+            )
+            acc = psum.tile([P, PIECE], F32, name="acc_0_%d" % h)
+            product(acc[:], 0, h)
+            y = y_first[:] if h == 0 else y_rest[:, (h - 1) * PIECE : h * PIECE]
+            nc.scalar.copy(y, acc[:])
+        acc_1 = psum.tile([P, S], F32, name="acc_1")
+        for h in reversed(range(PIECES)):
+            product(acc_1[:, pieces[h]], 1, h)
+        y_1 = keep.tile([P, S], F32, name="y_1")
+        nc.scalar.copy(y_1[:], acc_1[:])
+
+        nc.vector.tensor_copy(windows[0][:].indirect(entries(slot_sb, 0, PIECE)), y_first[:])
+        nc.vector.tensor_copy(windows[0][:].indirect(entries(slot_sb, PIECE, S)), y_rest[:])
+        nc.sync.dma_start(out[0:P, :], windows[0][:])
+        nc.vector.tensor_copy(windows[1][:].indirect(slot_sb[:]), y_1[:])
+        nc.sync.dma_start(out[P:N, :], windows[1][:])

@@ -60,27 +60,27 @@ def tile_picked_kvput_none_e_kernel(tc, xT, mem, w1_words, w1_scales, offs, slot
         def entries(tile, a, b):
             return tile[:, a // LIST_ROWS : b // LIST_ROWS]
 
-        woven = keep.tile([P, PIECES, PASSES, PIECE, PACK], BF16, name="woven", align_bytes=64)
         pieces = [slice(h * PIECE, (h + 1) * PIECE) for h in range(PIECES)]
+        woven = keep.tile([P, PASSES * S * PACK], BF16, name="woven", align_bytes=64)
+        woven_words = woven[:].bitcast(U32).rearrange("p (h z c u) -> p h z c u", h=PIECES, z=PASSES, u=2)
+        paired = [keep.tile([P, S * PACK], BF16, name="paired_%d" % z) for z in range(PASSES)]
 
-        for z, u in ((0, 0), (0, 1), (1, 0)):
-            pair = keep.tile([P, 2, S], F32, name="pair_%d_%d" % (z, u))
-            for e in range(2):
-                nc.vector.tensor_copy(pair[:, e, :], planes[z, 2 * u + e][:].indirect(offs_sb[:]))
-            nc.scalar.copy(
-                woven[:, :, z, :, 2 * u : 2 * u + 2],
-                pair[:].rearrange("p e (h c) -> p h c e", h=PIECES),
-            )
+        def gather(z, t, a, b):
+            dst = paired[z][:].rearrange("p (u c e) -> p u c e", u=2, e=2)[:, t // 2, a:b, t % 2]
+            nc.vector.tensor_copy(dst, planes[z, t][:].indirect(entries(offs_sb, a, b)))
 
-        last = keep.tile([P, 2, S], F32, name="last")
-        nc.vector.tensor_copy(last[:, 0, :], planes[1, 2][:].indirect(offs_sb[:]))
+        def words(z):
+            return paired[z][:].bitcast(U32).rearrange("p (u h c) -> p h c u", u=2, h=PIECES)
+
+        for t in range(PACK):
+            gather(0, t, 0, S)
+        nc.scalar.copy(woven_words[:, :, 0], words(0))
+        for t in range(PACK - 1):
+            gather(1, t, 0, S)
         for h in range(PIECES):
-            nc.vector.tensor_copy(
-                last[:, 1, pieces[h]],
-                planes[1, 3][:].indirect(entries(offs_sb, h * PIECE, (h + 1) * PIECE)),
-            )
+            gather(1, PACK - 1, h * PIECE, (h + 1) * PIECE)
         for h in range(PIECES):
-            nc.scalar.copy(woven[:, h, 1, :, 2:4], last[:, :, pieces[h]].rearrange("p e c -> p c e"))
+            nc.scalar.copy(woven_words[:, h, 1], words(1)[:, h])
 
         codes = keep.tile([P, PIECES, PASSES, PIECE], U32, name="codes", align_bytes=64)
         scales = keep.tile([P, PIECES, PASSES, PIECE], U8, name="scales", align_bytes=64)
@@ -103,7 +103,7 @@ def tile_picked_kvput_none_e_kernel(tc, xT, mem, w1_words, w1_scales, offs, slot
             nc.vector.quantize_mx(
                 out=codes[:, h].rearrange("p z c -> p (z c)").bitcast(FP8X4),
                 scales=scales[:, h].rearrange("p z c -> p (z c)"),
-                in_=woven[:, h].rearrange("p z c t -> p (z c t)"),
+                in_=woven[:, h * PASSES * PIECE * PACK : (h + 1) * PASSES * PIECE * PACK],
             )
             acc = psum.tile([P, PIECE], F32, name="acc_0_%d" % h)
             product(acc[:], 0, h)

@@ -11,6 +11,7 @@ I32 = mybir.dt.int32
 U32 = mybir.dt.uint32
 U16 = mybir.dt.uint16
 U8 = mybir.dt.uint8
+COPY = mybir.ActivationFunctionType.Copy
 FP8X4 = mybir.dt.float8_e4m3fn_x4
 
 P = 128
@@ -61,57 +62,68 @@ def tile_picked_kvput_none_e_kernel(tc, xT, mem, w1_words, w1_scales, offs, slot
             return tile[:, a // LIST_ROWS : b // LIST_ROWS]
 
         pieces = [slice(h * PIECE, (h + 1) * PIECE) for h in range(PIECES)]
-        woven = keep.tile([P, PASSES * S * PACK], BF16, name="woven", align_bytes=64)
-        woven_words = woven[:].bitcast(U32).rearrange("p (h z c u) -> p h z c u", h=PIECES, z=PASSES, u=2)
         paired = [keep.tile([P, S * PACK], BF16, name="paired_%d" % z) for z in range(PASSES)]
+        woven = [keep.tile([P, S * PACK], BF16, name="woven_%d" % z, align_bytes=64) for z in range(PASSES)]
+        codes = [keep.tile([P, S], U32, name="codes_%d" % z, align_bytes=64) for z in range(PASSES)]
+        scales = [keep.tile([P, S], U8, name="scales_%d" % z, align_bytes=64) for z in range(PASSES)]
+
+        def pair_slot(z, t, a, b):
+            return paired[z][:].rearrange("p (u c e) -> p u c e", u=2, e=2)[:, t // 2, a:b, t % 2]
 
         def gather(z, t, a, b):
-            dst = paired[z][:].rearrange("p (u c e) -> p u c e", u=2, e=2)[:, t // 2, a:b, t % 2]
-            nc.vector.tensor_copy(dst, planes[z, t][:].indirect(entries(offs_sb, a, b)))
+            nc.vector.tensor_copy(pair_slot(z, t, a, b), planes[z, t][:].indirect(entries(offs_sb, a, b)))
 
-        def words(z):
-            return paired[z][:].bitcast(U32).rearrange("p (u h c) -> p h c u", u=2, h=PIECES)
+        def weave(z, a, b):
+            nc.scalar.copy(
+                woven[z][:].bitcast(U32).rearrange("p (c u) -> p c u", u=2)[:, a:b, :],
+                paired[z][:].bitcast(U32).rearrange("p (u c) -> p c u", u=2)[:, a:b, :],
+            )
 
-        for t in range(PACK):
-            gather(0, t, 0, S)
-        nc.scalar.copy(woven_words[:, :, 0], words(0))
-        for t in range(PACK - 1):
-            gather(1, t, 0, S)
-        for h in range(PIECES):
-            gather(1, PACK - 1, h * PIECE, (h + 1) * PIECE)
-        for h in range(PIECES):
-            nc.scalar.copy(woven_words[:, h, 1], words(1)[:, h])
+        def quantise(z, a, b):
+            nc.vector.quantize_mx(
+                out=codes[z][:, a:b].bitcast(FP8X4),
+                scales=scales[z][:, a:b],
+                in_=woven[z][:, a * PACK : b * PACK],
+            )
 
-        codes = keep.tile([P, PIECES, PASSES, PIECE], U32, name="codes", align_bytes=64)
-        scales = keep.tile([P, PIECES, PASSES, PIECE], U8, name="scales", align_bytes=64)
-
-        def product(acc, m, h):
+        def product(acc, m, a, b):
             for z in range(PASSES):
                 nc.tensor.matmul_mx(
                     out=acc,
                     lhsT=w_words[:, z, m * P : (m + 1) * P].bitcast(FP8X4),
                     lhsT_scale=w_scales[:, z, m * P : (m + 1) * P],
-                    rhs=codes[:, h, z, :].bitcast(FP8X4),
-                    rhs_scale=scales[:, h, z, :],
+                    rhs=codes[z][:, a:b].bitcast(FP8X4),
+                    rhs_scale=scales[z][:, a:b],
                     start=(z == 0),
                     stop=(z == PASSES - 1),
                 )
 
+        for t in range(PACK):
+            gather(0, t, 0, S)
+        for a in (0, S // 2):
+            weave(0, a, a + S // 2)
+        for t in range(2):
+            rounded = keep.tile([P, T], BF16, name="rounded_%d" % t)
+            nc.vector.tensor_copy(rounded[:], planes[1, t][:])
+            nc.scalar.activation(pair_slot(1, t, 0, S), rounded[:].indirect(offs_sb[:]), COPY)
+        for a in (0, S // 2):
+            quantise(0, a, a + S // 2)
+        gather(1, 2, 0, S)
+        for h in range(PIECES):
+            gather(1, 3, h * PIECE, (h + 1) * PIECE)
+        for h in range(PIECES):
+            weave(1, h * PIECE, (h + 1) * PIECE)
+
         y_first = keep.tile([P, PIECE], F32, name="y_first")
         y_rest = keep.tile([P, S - PIECE], F32, name="y_rest")
         for h in range(PIECES):
-            nc.vector.quantize_mx(
-                out=codes[:, h].rearrange("p z c -> p (z c)").bitcast(FP8X4),
-                scales=scales[:, h].rearrange("p z c -> p (z c)"),
-                in_=woven[:, h * PASSES * PIECE * PACK : (h + 1) * PASSES * PIECE * PACK],
-            )
+            quantise(1, h * PIECE, (h + 1) * PIECE)
             acc = psum.tile([P, PIECE], F32, name="acc_0_%d" % h)
-            product(acc[:], 0, h)
+            product(acc[:], 0, h * PIECE, (h + 1) * PIECE)
             y = y_first[:] if h == 0 else y_rest[:, (h - 1) * PIECE : h * PIECE]
             nc.scalar.copy(y, acc[:])
         acc_1 = psum.tile([P, S], F32, name="acc_1")
-        for h in reversed(range(PIECES)):
-            product(acc_1[:, pieces[h]], 1, h)
+        product(acc_1[:], 1, 0, S)
         y_1 = keep.tile([P, S], F32, name="y_1")
         nc.scalar.copy(y_1[:], acc_1[:])
 

@@ -32,7 +32,7 @@ def tile_picked_kvput_none_e_kernel(tc, xT, mem, w1_words, w1_scales, offs, slot
 
         offs_sb = keep.tile([P, S // LIST_ROWS], U16, name="offs_sb")
         slot_sb = keep.tile([P, S // LIST_ROWS], U16, name="slot_sb")
-        w_words = keep.tile([P, PASSES, N], U32, name="w_words", align_bytes=64)
+        w_words = [keep.tile([P, PASSES, P], U32, name="w_words_%d" % m, align_bytes=64) for m in range(BLOCKS)]
         w_scales = keep.tile([P, PASSES, N], U8, name="w_scales", align_bytes=64)
         nc.vector.memset(w_scales[:].bitcast(I32), 0)
 
@@ -44,19 +44,16 @@ def tile_picked_kvput_none_e_kernel(tc, xT, mem, w1_words, w1_scales, offs, slot
                 nc.sync.dma_start(planes[z, t][:], x_rows[z, t])
                 if (z, t) == (0, 0):
                     nc.sync.dma_start(offs_sb[:], offs)
-        nc.sync.dma_start(
-            w_words[:].bitcast(I32),
-            w1_words.rearrange("z p n r -> p z (n r)").bitcast(I32),
-        )
+        w_rows = w1_words.rearrange("z p n r -> p z (n r)").bitcast(I32)
         scale_rows = w1_scales.bitcast(I32).rearrange("z (q i) c -> i q z c", i=4)
+        windows = [keep.tile([P, U], F32, name="window_%d" % m) for m in range(BLOCKS)]
+        nc.sync.dma_start(w_words[0][:].bitcast(I32), w_rows[:, :, 0:P])
         for i in range(4):
             nc.sync.dma_start(w_scales[:].bitcast(I32)[i:P:32], scale_rows[i])
+        nc.sync.dma_start(windows[0][:], mem[0:P, :])
         nc.sync.dma_start(slot_sb[:], slot)
-        windows = []
-        for m in range(BLOCKS):
-            window = keep.tile([P, U], F32, name="window_%d" % m)
-            nc.sync.dma_start(window[:], mem[m * P : (m + 1) * P, :])
-            windows.append(window)
+        nc.sync.dma_start(w_words[1][:].bitcast(I32), w_rows[:, :, P:N])
+        nc.sync.dma_start(windows[1][:], mem[P:N, :])
 
         def entries(tile, a, b):
             return tile[:, a // LIST_ROWS : b // LIST_ROWS]
@@ -90,7 +87,7 @@ def tile_picked_kvput_none_e_kernel(tc, xT, mem, w1_words, w1_scales, offs, slot
             for z in range(PASSES):
                 nc.tensor.matmul_mx(
                     out=acc,
-                    lhsT=w_words[:, z, m * P : (m + 1) * P].bitcast(FP8X4),
+                    lhsT=w_words[m][:, z, :].bitcast(FP8X4),
                     lhsT_scale=w_scales[:, z, m * P : (m + 1) * P],
                     rhs=codes[z][:, a:b].bitcast(FP8X4),
                     rhs_scale=scales[z][:, a:b],

@@ -58,11 +58,16 @@ def tile_picked_kvput_none_e_kernel(tc, xT, mem, w1_words, w1_scales, offs, slot
         def entries(tile, a, b):
             return tile[:, a // LIST_ROWS : b // LIST_ROWS]
 
-        pieces = [slice(h * PIECE, (h + 1) * PIECE) for h in range(PIECES)]
+        HALF = S // 2
         paired = [keep.tile([P, S * PACK], BF16, name="paired_%d" % z) for z in range(PASSES)]
-        woven = [keep.tile([P, S * PACK], BF16, name="woven_%d" % z, align_bytes=64) for z in range(PASSES)]
-        codes = [keep.tile([P, S], U32, name="codes_%d" % z, align_bytes=64) for z in range(PASSES)]
-        scales = [keep.tile([P, S], U8, name="scales_%d" % z, align_bytes=64) for z in range(PASSES)]
+        woven = keep.tile([P, PASSES * S * PACK], BF16, name="woven", align_bytes=64)
+        codes = keep.tile([P, PASSES * S], U32, name="codes", align_bytes=64)
+        scales = keep.tile([P, PASSES * S], U8, name="scales", align_bytes=64)
+
+        def place(z, a):
+            if a < HALF:
+                return z * HALF + a
+            return S + (a - HALF) // PIECE * PASSES * PIECE + z * PIECE
 
         def pair_slot(z, t, a, b):
             return paired[z][:].rearrange("p (u c e) -> p u c e", u=2, e=2)[:, t // 2, a:b, t % 2]
@@ -70,57 +75,69 @@ def tile_picked_kvput_none_e_kernel(tc, xT, mem, w1_words, w1_scales, offs, slot
         def gather(z, t, a, b):
             nc.vector.tensor_copy(pair_slot(z, t, a, b), planes[z, t][:].indirect(entries(offs_sb, a, b)))
 
+        def round_plane(z, t):
+            rounded = keep.tile([P, T], BF16, name="rounded_%d_%d" % (z, t))
+            nc.vector.tensor_copy(rounded[:], planes[z, t][:])
+            return rounded
+
         def weave(z, a, b):
+            at = place(z, a)
             nc.scalar.copy(
-                woven[z][:].bitcast(U32).rearrange("p (c u) -> p c u", u=2)[:, a:b, :],
+                woven[:].bitcast(U32).rearrange("p (c u) -> p c u", u=2)[:, at : at + b - a, :],
                 paired[z][:].bitcast(U32).rearrange("p (u c) -> p c u", u=2)[:, a:b, :],
             )
 
-        def quantise(z, a, b):
+        def quantise(at, n):
             nc.vector.quantize_mx(
-                out=codes[z][:, a:b].bitcast(FP8X4),
-                scales=scales[z][:, a:b],
-                in_=woven[z][:, a * PACK : b * PACK],
+                out=codes[:, at : at + n].bitcast(FP8X4),
+                scales=scales[:, at : at + n],
+                in_=woven[:, at * PACK : (at + n) * PACK],
             )
 
         def product(acc, m, a, b):
             for z in range(PASSES):
+                at = place(z, a)
                 nc.tensor.matmul_mx(
                     out=acc,
                     lhsT=w_words[m][:, z, :].bitcast(FP8X4),
                     lhsT_scale=w_scales[:, z, m * P : (m + 1) * P],
-                    rhs=codes[z][:, a:b].bitcast(FP8X4),
-                    rhs_scale=scales[z][:, a:b],
+                    rhs=codes[:, at : at + b - a].bitcast(FP8X4),
+                    rhs_scale=scales[:, at : at + b - a],
                     start=(z == 0),
                     stop=(z == PASSES - 1),
                 )
 
         for t in range(PACK):
             gather(0, t, 0, S)
-        for a in (0, S // 2):
-            weave(0, a, a + S // 2)
-        for t in range(2):
-            rounded = keep.tile([P, T], BF16, name="rounded_%d" % t)
-            nc.vector.tensor_copy(rounded[:], planes[1, t][:])
-            nc.scalar.activation(pair_slot(1, t, 0, S), rounded[:].indirect(offs_sb[:]), COPY)
-        for a in (0, S // 2):
-            quantise(0, a, a + S // 2)
+        weave(0, 0, HALF)
+        nc.scalar.copy(
+            woven[:].bitcast(U32)[:, 2 * S : 4 * S].rearrange("p (h z c u) -> p h z c u", h=2, z=PASSES, u=2)[:, :, 0],
+            paired[0][:].bitcast(U32).rearrange("p (u h c) -> p h c u", u=2, h=PIECES)[:, 2:4],
+        )
+        gather(1, 0, 0, S)
+        nc.scalar.activation(pair_slot(1, 1, 0, S), round_plane(1, 1)[:].indirect(offs_sb[:]), COPY)
+        quantise(place(0, 0), HALF)
         gather(1, 2, 0, S)
-        for h in range(PIECES):
-            gather(1, 3, h * PIECE, (h + 1) * PIECE)
-        for h in range(PIECES):
-            weave(1, h * PIECE, (h + 1) * PIECE)
+        for a in range(0, S, PIECE):
+            gather(1, 3, a, a + PIECE)
+        for a in range(0, S, PIECE):
+            weave(1, a, a + PIECE)
 
         y_first = keep.tile([P, PIECE], F32, name="y_first")
         y_rest = keep.tile([P, S - PIECE], F32, name="y_rest")
         for h in range(PIECES):
-            quantise(1, h * PIECE, (h + 1) * PIECE)
+            a = h * PIECE
+            if a >= HALF:
+                quantise(place(0, a), PASSES * PIECE)
+            else:
+                quantise(place(1, a), PIECE)
             acc = psum.tile([P, PIECE], F32, name="acc_0_%d" % h)
-            product(acc[:], 0, h * PIECE, (h + 1) * PIECE)
-            y = y_first[:] if h == 0 else y_rest[:, (h - 1) * PIECE : h * PIECE]
+            product(acc[:], 0, a, a + PIECE)
+            y = y_first[:] if h == 0 else y_rest[:, a - PIECE : a]
             nc.scalar.copy(y, acc[:])
         acc_1 = psum.tile([P, S], F32, name="acc_1")
-        product(acc_1[:], 1, 0, S)
+        for a, b in ((384, 512), (256, 384), (0, 256)):
+            product(acc_1[:, a:b], 1, a, b)
         y_1 = keep.tile([P, S], F32, name="y_1")
         nc.scalar.copy(y_1[:], acc_1[:])
 

@@ -49,7 +49,7 @@ def tile_picked_kvput_none_e_kernel(tc, xT, mem, w1_words, w1_scales, offs, slot
         windows = [keep.tile([P, U], F32, name="window_%d" % m) for m in range(BLOCKS)]
         nc.sync.dma_start(w_words[0][:].bitcast(I32), w_rows[:, :, 0:P])
         for i in range(4):
-            nc.sync.dma_start(w_scales[:].bitcast(I32)[i:P:32], scale_rows[i])
+            nc.scalar.dma_start(w_scales[:].bitcast(I32)[i:P:32], scale_rows[i])
         nc.sync.dma_start(windows[0][:], mem[0:P, :])
         nc.sync.dma_start(slot_sb[:], slot)
         nc.sync.dma_start(w_words[1][:].bitcast(I32), w_rows[:, :, P:N])

@@ -123,26 +123,31 @@ def tile_picked_kvput_none_e_kernel(tc, xT, mem, w1_words, w1_scales, offs, slot
         for a in range(0, S, PIECE):
             weave(1, a, a + PIECE)
 
-        y_first = keep.tile([P, PIECE], F32, name="y_first")
-        y_rest = keep.tile([P, S - PIECE], F32, name="y_rest")
+        y_early = keep.tile([P, HALF], F32, name="y_early")
+        y_late = keep.tile([P, HALF], F32, name="y_late")
+        y_1 = keep.tile([P, S], F32, name="y_1")
         for h in range(PIECES):
             a = h * PIECE
             if a >= HALF:
                 quantise(place(0, a), PASSES * PIECE)
             else:
                 quantise(place(1, a), PIECE)
-            acc = psum.tile([P, PIECE], F32, name="acc_0_%d" % h)
-            product(acc[:], 0, a, a + PIECE)
-            y = y_first[:] if h == 0 else y_rest[:, a - PIECE : a]
-            nc.scalar.copy(y, acc[:])
-        acc_1 = psum.tile([P, S], F32, name="acc_1")
-        for a, b in ((384, 512), (256, 384), (0, 256)):
-            product(acc_1[:, a:b], 1, a, b)
-        y_1 = keep.tile([P, S], F32, name="y_1")
-        nc.scalar.copy(y_1[:], acc_1[:])
-
-        nc.vector.tensor_copy(windows[0][:].indirect(entries(slot_sb, 0, PIECE)), y_first[:])
-        nc.vector.tensor_copy(windows[0][:].indirect(entries(slot_sb, PIECE, S)), y_rest[:])
-        nc.sync.dma_start(out[0:P, :], windows[0][:])
+                acc = psum.tile([P, PIECE], F32, name="acc_0_%d" % h)
+                product(acc[:], 0, a, a + PIECE)
+                nc.scalar.copy(y_early[:, a : a + PIECE], acc[:])
+        nc.vector.tensor_copy(windows[0][:].indirect(entries(slot_sb, 0, HALF)), y_early[:])
+        acc_1 = psum.tile([P, HALF], F32, name="acc_1")
+        product(acc_1[:], 1, 0, HALF)
+        nc.scalar.copy(y_1[:, 0:HALF], acc_1[:])
+        acc_late = psum.tile([P, HALF], F32, name="acc_late_1", tag="late")
+        for a in (HALF + PIECE, HALF):
+            product(acc_late[:, a - HALF : a - HALF + PIECE], 1, a, a + PIECE)
+        nc.scalar.copy(y_1[:, HALF:S], acc_late[:])
+        for a in (HALF, HALF + PIECE):
+            acc_late = psum.tile([P, HALF], F32, name="acc_late_0", tag="late")
+            product(acc_late[:, 0:PIECE], 0, a, a + PIECE)
+            nc.scalar.copy(y_late[:, a - HALF : a - HALF + PIECE], acc_late[:, 0:PIECE])
         nc.vector.tensor_copy(windows[1][:].indirect(slot_sb[:]), y_1[:])
         nc.sync.dma_start(out[P:N, :], windows[1][:])
+        nc.vector.tensor_copy(windows[0][:].indirect(entries(slot_sb, HALF, S)), y_late[:])
+        nc.sync.dma_start(out[0:P, :], windows[0][:])

@@ -16,12 +16,14 @@ FP8X4 = mybir.dt.float8_e4m3fn_x4
 
 P = 128
 PACK = 4
-K_PASS = P * PACK
-PASSES = K // K_PASS
-BLOCKS = N // P
+PASSES = K // (P * PACK)
+ROW_BLOCKS = N // P
 LIST_ROWS = 16
+QUADRANT = 32
+SCALE_ROWS = 4
 PIECE = 128
 PIECES = S // PIECE
+HALF = S // 2
 
 
 def tile_picked_kvput_none_e_kernel(tc, xT, mem, w1_words, w1_scales, offs, slot, out):
@@ -32,7 +34,7 @@ def tile_picked_kvput_none_e_kernel(tc, xT, mem, w1_words, w1_scales, offs, slot
 
         offs_sb = keep.tile([P, S // LIST_ROWS], U16, name="offs_sb")
         slot_sb = keep.tile([P, S // LIST_ROWS], U16, name="slot_sb")
-        w_words = [keep.tile([P, PASSES, P], U32, name="w_words_%d" % m, align_bytes=64) for m in range(BLOCKS)]
+        w_words = [keep.tile([P, PASSES, P], U32, name="w_words_%d" % m, align_bytes=64) for m in range(ROW_BLOCKS)]
         w_scales = keep.tile([P, PASSES, N], U8, name="w_scales", align_bytes=64)
         nc.vector.memset(w_scales[:].bitcast(I32), 0)
 
@@ -45,20 +47,19 @@ def tile_picked_kvput_none_e_kernel(tc, xT, mem, w1_words, w1_scales, offs, slot
                 if (z, t) == (0, 0):
                     nc.sync.dma_start(offs_sb[:], offs)
         w_rows = w1_words.rearrange("z p n r -> p z (n r)").bitcast(I32)
-        scale_rows = w1_scales.bitcast(I32).rearrange("z (q i) c -> i q z c", i=4)
-        windows = [keep.tile([P, U], F32, name="window_%d" % m) for m in range(BLOCKS)]
+        scale_rows = w1_scales.bitcast(I32).rearrange("z (q i) c -> i q z c", i=SCALE_ROWS)
+        windows = [keep.tile([P, U], F32, name="window_%d" % m) for m in range(ROW_BLOCKS)]
         nc.sync.dma_start(w_words[0][:].bitcast(I32), w_rows[:, :, 0:P])
-        for i in range(4):
-            nc.scalar.dma_start(w_scales[:].bitcast(I32)[i:P:32], scale_rows[i])
+        for i in range(SCALE_ROWS):
+            nc.scalar.dma_start(w_scales[:].bitcast(I32)[i:P:QUADRANT], scale_rows[i])
         nc.sync.dma_start(windows[0][:], mem[0:P, :])
         nc.sync.dma_start(slot_sb[:], slot)
         nc.sync.dma_start(w_words[1][:].bitcast(I32), w_rows[:, :, P:N])
         nc.sync.dma_start(windows[1][:], mem[P:N, :])
 
-        def entries(tile, a, b):
-            return tile[:, a // LIST_ROWS : b // LIST_ROWS]
+        def entries(list_tile, a, b):
+            return list_tile[:, a // LIST_ROWS : b // LIST_ROWS]
 
-        HALF = S // 2
         paired = [keep.tile([P, S * PACK], BF16, name="paired_%d" % z) for z in range(PASSES)]
         woven = keep.tile([P, PASSES * S * PACK], BF16, name="woven", align_bytes=64)
         codes = keep.tile([P, PASSES * S], U32, name="codes", align_bytes=64)
@@ -74,11 +75,6 @@ def tile_picked_kvput_none_e_kernel(tc, xT, mem, w1_words, w1_scales, offs, slot
 
         def gather(z, t, a, b):
             nc.vector.tensor_copy(pair_slot(z, t, a, b), planes[z, t][:].indirect(entries(offs_sb, a, b)))
-
-        def round_plane(z, t):
-            rounded = keep.tile([P, T], BF16, name="rounded_%d_%d" % (z, t))
-            nc.vector.tensor_copy(rounded[:], planes[z, t][:])
-            return rounded
 
         def weave(z, a, b):
             at = place(z, a)
@@ -112,10 +108,13 @@ def tile_picked_kvput_none_e_kernel(tc, xT, mem, w1_words, w1_scales, offs, slot
         weave(0, 0, HALF)
         nc.scalar.copy(
             woven[:].bitcast(U32)[:, 2 * S : 4 * S].rearrange("p (h z c u) -> p h z c u", h=2, z=PASSES, u=2)[:, :, 0],
-            paired[0][:].bitcast(U32).rearrange("p (u h c) -> p h c u", u=2, h=PIECES)[:, 2:4],
+            paired[0][:].bitcast(U32).rearrange("p (u h c) -> p h c u", u=2, h=PIECES)[:, PIECES // 2 : PIECES],
         )
+
         gather(1, 0, 0, S)
-        nc.scalar.activation(pair_slot(1, 1, 0, S), round_plane(1, 1)[:].indirect(offs_sb[:]), COPY)
+        rounded = keep.tile([P, T], BF16, name="rounded")
+        nc.vector.tensor_copy(rounded[:], planes[1, 1][:])
+        nc.scalar.activation(pair_slot(1, 1, 0, S), rounded[:].indirect(offs_sb[:]), COPY)
         quantise(place(0, 0), HALF)
         gather(1, 2, 0, S)
         for a in range(0, S, PIECE):
@@ -125,29 +124,29 @@ def tile_picked_kvput_none_e_kernel(tc, xT, mem, w1_words, w1_scales, offs, slot
 
         y_early = keep.tile([P, HALF], F32, name="y_early")
         y_late = keep.tile([P, HALF], F32, name="y_late")
-        y_1 = keep.tile([P, S], F32, name="y_1")
-        for h in range(PIECES):
-            a = h * PIECE
-            if a >= HALF:
-                quantise(place(0, a), PASSES * PIECE)
-            else:
-                quantise(place(1, a), PIECE)
-                acc = psum.tile([P, PIECE], F32, name="acc_0_%d" % h)
-                product(acc[:], 0, a, a + PIECE)
-                nc.scalar.copy(y_early[:, a : a + PIECE], acc[:])
+        y_block_1 = keep.tile([P, S], F32, name="y_block_1")
+        for a in range(0, HALF, PIECE):
+            quantise(place(1, a), PIECE)
+            acc = psum.tile([P, PIECE], F32, name="acc_early_0_%d" % a)
+            product(acc[:], 0, a, a + PIECE)
+            nc.scalar.copy(y_early[:, a : a + PIECE], acc[:])
+        for a in range(HALF, S, PIECE):
+            quantise(place(0, a), PASSES * PIECE)
         nc.vector.tensor_copy(windows[0][:].indirect(entries(slot_sb, 0, HALF)), y_early[:])
-        acc_1 = psum.tile([P, HALF], F32, name="acc_1")
-        product(acc_1[:], 1, 0, HALF)
-        nc.scalar.copy(y_1[:, 0:HALF], acc_1[:])
-        acc_late = psum.tile([P, HALF], F32, name="acc_late_1", tag="late")
-        for a in (HALF + PIECE, HALF):
-            product(acc_late[:, a - HALF : a - HALF + PIECE], 1, a, a + PIECE)
-        nc.scalar.copy(y_1[:, HALF:S], acc_late[:])
-        for a in (HALF, HALF + PIECE):
-            acc_late = psum.tile([P, HALF], F32, name="acc_late_0", tag="late")
-            product(acc_late[:, 0:PIECE], 0, a, a + PIECE)
-            nc.scalar.copy(y_late[:, a - HALF : a - HALF + PIECE], acc_late[:, 0:PIECE])
-        nc.vector.tensor_copy(windows[1][:].indirect(slot_sb[:]), y_1[:])
+
+        acc = psum.tile([P, HALF], F32, name="acc_early_1")
+        product(acc[:], 1, 0, HALF)
+        nc.scalar.copy(y_block_1[:, 0:HALF], acc[:])
+        acc = psum.tile([P, HALF], F32, name="acc_late_1", tag="late")
+        for a in range(HALF, S, PIECE):
+            product(acc[:, a - HALF : a - HALF + PIECE], 1, a, a + PIECE)
+        nc.scalar.copy(y_block_1[:, HALF:S], acc[:])
+        for a in range(HALF, S, PIECE):
+            acc = psum.tile([P, HALF], F32, name="acc_late_0", tag="late")
+            product(acc[:, 0:PIECE], 0, a, a + PIECE)
+            nc.scalar.copy(y_late[:, a - HALF : a - HALF + PIECE], acc[:, 0:PIECE])
+
+        nc.vector.tensor_copy(windows[1][:].indirect(slot_sb[:]), y_block_1[:])
         nc.sync.dma_start(out[P:N, :], windows[1][:])
         nc.vector.tensor_copy(windows[0][:].indirect(entries(slot_sb, HALF, S)), y_late[:])
         nc.sync.dma_start(out[0:P, :], windows[0][:])

@@ -21,9 +21,10 @@ ROW_BLOCKS = N // P
 LIST_ROWS = 16
 QUADRANT = 32
 SCALE_ROWS = 4
+ROW_ALIGN = 256
 PIECE = 128
-PIECES = S // PIECE
-HALF = S // 2
+SCALAR_SHARE = (256, 320)
+PIECES = ((0, 128), (128, 256), (256, 512))
 
 
 def tile_picked_kvput_none_e_kernel(tc, xT, mem, w1_words, w1_scales, offs, slot, out):
@@ -32,121 +33,101 @@ def tile_picked_kvput_none_e_kernel(tc, xT, mem, w1_words, w1_scales, offs, slot
         keep = ctx.enter_context(tc.tile_pool(name="keep", bufs=1))
         psum = ctx.enter_context(tc.psum_pool(name="psum", bufs=1))
 
-        offs_sb = keep.tile([P, S // LIST_ROWS], U16, name="offs_sb")
-        slot_sb = keep.tile([P, S // LIST_ROWS], U16, name="slot_sb")
-        w_words = [keep.tile([P, PASSES, P], U32, name="w_words_%d" % m, align_bytes=64) for m in range(ROW_BLOCKS)]
-        w_scales = keep.tile([P, PASSES, N], U8, name="w_scales", align_bytes=64)
+        offs_sb = keep.tile([P, S // LIST_ROWS], U16, name="offs_sb", align_bytes=ROW_ALIGN)
+        slot_sb = keep.tile([P, S // LIST_ROWS], U16, name="slot_sb", align_bytes=ROW_ALIGN)
+        w_words = [keep.tile([P, N], U32, name="w_words_%d" % z, align_bytes=ROW_ALIGN) for z in range(PASSES)]
+        w_scales = keep.tile([P, PASSES, N], U8, name="w_scales", align_bytes=ROW_ALIGN)
+        staged = keep.tile([SCALE_ROWS, PASSES, P // QUADRANT, N // 4], I32, name="staged", align_bytes=ROW_ALIGN)
         nc.vector.memset(w_scales[:].bitcast(I32), 0)
+        nc.scalar.dma_start(
+            staged[:].rearrange("i z q c -> i (z q) c"),
+            w1_scales.bitcast(I32).rearrange("z (q i) c -> i (z q) c", i=SCALE_ROWS),
+        )
+        nc.scalar.copy(w_scales[:].bitcast(U32)[0:SCALE_ROWS], staged[:, :, 0, :].bitcast(U32))
+        for q in range(1, P // QUADRANT):
+            nc.vector.tensor_copy(
+                w_scales[:].bitcast(I32)[q * QUADRANT : q * QUADRANT + SCALE_ROWS], staged[:, :, q, :]
+            )
 
         x_rows = xT.rearrange("(z p t) c -> z t p c", z=PASSES, t=PACK)
+        w_rows = w1_words.rearrange("z p n r -> z p (n r)").bitcast(I32)
         planes = {}
         for z in range(PASSES):
             for t in range(PACK):
-                planes[z, t] = keep.tile([P, T], F32, name="plane_%d_%d" % (z, t))
+                planes[z, t] = keep.tile([P, T], F32, name="plane_%d_%d" % (z, t), align_bytes=ROW_ALIGN)
+                if (z, t) == (PASSES - 1, PACK - 1):
+                    nc.sync.dma_start(w_words[0][:].bitcast(I32), w_rows[0])
                 nc.sync.dma_start(planes[z, t][:], x_rows[z, t])
                 if (z, t) == (0, 0):
                     nc.sync.dma_start(offs_sb[:], offs)
-        w_rows = w1_words.rearrange("z p n r -> p z (n r)").bitcast(I32)
-        scale_rows = w1_scales.bitcast(I32).rearrange("z (q i) c -> i q z c", i=SCALE_ROWS)
-        windows = [keep.tile([P, U], F32, name="window_%d" % m) for m in range(ROW_BLOCKS)]
-        nc.sync.dma_start(w_words[0][:].bitcast(I32), w_rows[:, :, 0:P])
-        for i in range(SCALE_ROWS):
-            nc.scalar.dma_start(w_scales[:].bitcast(I32)[i:P:QUADRANT], scale_rows[i])
+        windows = [keep.tile([P, U], F32, name="window_%d" % m, align_bytes=ROW_ALIGN) for m in range(ROW_BLOCKS)]
+        nc.sync.dma_start(w_words[1][:].bitcast(I32), w_rows[1])
         nc.sync.dma_start(windows[0][:], mem[0:P, :])
         nc.sync.dma_start(slot_sb[:], slot)
-        nc.sync.dma_start(w_words[1][:].bitcast(I32), w_rows[:, :, P:N])
         nc.sync.dma_start(windows[1][:], mem[P:N, :])
 
         def entries(list_tile, a, b):
             return list_tile[:, a // LIST_ROWS : b // LIST_ROWS]
 
-        paired = [keep.tile([P, S * PACK], BF16, name="paired_%d" % z) for z in range(PASSES)]
-        woven = keep.tile([P, PASSES * S * PACK], BF16, name="woven", align_bytes=64)
-        codes = keep.tile([P, PASSES * S], U32, name="codes", align_bytes=64)
-        scales = keep.tile([P, PASSES * S], U8, name="scales", align_bytes=64)
+        woven = [keep.tile([P, S * PACK], BF16, name="woven_%d" % z, align_bytes=64) for z in range(PASSES)]
+        codes = [keep.tile([P, S], U32, name="codes_%d" % z, align_bytes=64) for z in range(PASSES)]
+        scales = [keep.tile([P, S], U8, name="scales_%d" % z, align_bytes=64) for z in range(PASSES)]
 
-        def place(z, a):
-            if a < HALF:
-                return z * HALF + a
-            return S + (a - HALF) // PIECE * PASSES * PIECE + z * PIECE
+        def picked(z, t, a, b):
+            return woven[z][:, a * PACK + t : b * PACK : PACK], planes[z, t][:].indirect(entries(offs_sb, a, b))
 
-        def pair_slot(z, t, a, b):
-            return paired[z][:].rearrange("p (u c e) -> p u c e", u=2, e=2)[:, t // 2, a:b, t % 2]
+        def gather_vector(z, t, a, b):
+            nc.vector.tensor_copy(*picked(z, t, a, b))
 
-        def gather(z, t, a, b):
-            nc.vector.tensor_copy(pair_slot(z, t, a, b), planes[z, t][:].indirect(entries(offs_sb, a, b)))
+        def gather_scalar(z, t, a, b):
+            nc.scalar.activation(*picked(z, t, a, b), COPY)
 
-        def weave(z, a, b):
-            at = place(z, a)
-            nc.scalar.copy(
-                woven[:].bitcast(U32).rearrange("p (c u) -> p c u", u=2)[:, at : at + b - a, :],
-                paired[z][:].bitcast(U32).rearrange("p (u c) -> p c u", u=2)[:, a:b, :],
-            )
-
-        def quantise(at, n):
+        def quantise(z, a, b):
             nc.vector.quantize_mx(
-                out=codes[:, at : at + n].bitcast(FP8X4),
-                scales=scales[:, at : at + n],
-                in_=woven[:, at * PACK : (at + n) * PACK],
+                out=codes[z][:, a:b].bitcast(FP8X4), scales=scales[z][:, a:b], in_=woven[z][:, a * PACK : b * PACK]
             )
 
-        def product(acc, m, a, b):
-            for z in range(PASSES):
-                at = place(z, a)
-                nc.tensor.matmul_mx(
-                    out=acc,
-                    lhsT=w_words[m][:, z, :].bitcast(FP8X4),
-                    lhsT_scale=w_scales[:, z, m * P : (m + 1) * P],
-                    rhs=codes[:, at : at + b - a].bitcast(FP8X4),
-                    rhs_scale=scales[:, at : at + b - a],
-                    start=(z == 0),
-                    stop=(z == PASSES - 1),
-                )
+        acc = {
+            (m, a): psum.tile([P, b - a], F32, name="acc_%d_%d" % (m, a)) for a, b in PIECES for m in range(ROW_BLOCKS)
+        }
+
+        def product(z, m, a, b):
+            nc.tensor.matmul_mx(
+                out=acc[m, a][:],
+                lhsT=w_words[z][:, m * P : (m + 1) * P].bitcast(FP8X4),
+                lhsT_scale=w_scales[:, z, m * P : (m + 1) * P],
+                rhs=codes[z][:, a:b].bitcast(FP8X4),
+                rhs_scale=scales[z][:, a:b],
+                start=(z == 0),
+                stop=(z == PASSES - 1),
+            )
 
         for t in range(PACK):
-            gather(0, t, 0, S)
-        weave(0, 0, HALF)
-        nc.scalar.copy(
-            woven[:].bitcast(U32)[:, 2 * S : 4 * S].rearrange("p (h z c u) -> p h z c u", h=2, z=PASSES, u=2)[:, :, 0],
-            paired[0][:].bitcast(U32).rearrange("p (u h c) -> p h c u", u=2, h=PIECES)[:, PIECES // 2 : PIECES],
-        )
+            gather_vector(0, t, SCALAR_SHARE[0], S)
+            gather_scalar(0, t, 0, SCALAR_SHARE[0])
+        quantise(0, 0, S)
+        for a, b in PIECES:
+            for m in range(ROW_BLOCKS):
+                product(0, m, a, b)
+        for t in range(PACK - 1):
+            gather_vector(1, t, SCALAR_SHARE[1], S)
+            gather_scalar(1, t, 0, SCALAR_SHARE[1])
+        gather_vector(1, PACK - 1, SCALAR_SHARE[1], S)
+        for a in range(0, SCALAR_SHARE[1], PIECE):
+            gather_scalar(1, PACK - 1, a, min(a + PIECE, SCALAR_SHARE[1]))
 
-        gather(1, 0, 0, S)
-        rounded = keep.tile([P, T], BF16, name="rounded")
-        nc.vector.tensor_copy(rounded[:], planes[1, 1][:])
-        nc.scalar.activation(pair_slot(1, 1, 0, S), rounded[:].indirect(offs_sb[:]), COPY)
-        quantise(place(0, 0), HALF)
-        gather(1, 2, 0, S)
-        for a in range(0, S, PIECE):
-            gather(1, 3, a, a + PIECE)
-        for a in range(0, S, PIECE):
-            weave(1, a, a + PIECE)
+        y = [keep.tile([P, S], F32, name="y_%d" % m) for m in range(ROW_BLOCKS)]
+        for a, b in PIECES:
+            quantise(1, a, b)
+            for m in range(ROW_BLOCKS):
+                product(1, m, a, b)
+                if a == 0:
+                    nc.scalar.copy(y[m][:, a:b], acc[m, a][:])
+                else:
+                    nc.vector.tensor_copy(y[m][:, a:b], acc[m, a][:])
 
-        y_early = keep.tile([P, HALF], F32, name="y_early")
-        y_late = keep.tile([P, HALF], F32, name="y_late")
-        y_block_1 = keep.tile([P, S], F32, name="y_block_1")
-        for a in range(0, HALF, PIECE):
-            quantise(place(1, a), PIECE)
-            acc = psum.tile([P, PIECE], F32, name="acc_early_0_%d" % a)
-            product(acc[:], 0, a, a + PIECE)
-            nc.scalar.copy(y_early[:, a : a + PIECE], acc[:])
-        for a in range(HALF, S, PIECE):
-            quantise(place(0, a), PASSES * PIECE)
-        nc.vector.tensor_copy(windows[0][:].indirect(entries(slot_sb, 0, HALF)), y_early[:])
-
-        acc = psum.tile([P, HALF], F32, name="acc_early_1")
-        product(acc[:], 1, 0, HALF)
-        nc.scalar.copy(y_block_1[:, 0:HALF], acc[:])
-        acc = psum.tile([P, HALF], F32, name="acc_late_1", tag="late")
-        for a in range(HALF, S, PIECE):
-            product(acc[:, a - HALF : a - HALF + PIECE], 1, a, a + PIECE)
-        nc.scalar.copy(y_block_1[:, HALF:S], acc[:])
-        for a in range(HALF, S, PIECE):
-            acc = psum.tile([P, HALF], F32, name="acc_late_0", tag="late")
-            product(acc[:, 0:PIECE], 0, a, a + PIECE)
-            nc.scalar.copy(y_late[:, a - HALF : a - HALF + PIECE], acc[:, 0:PIECE])
-
-        nc.vector.tensor_copy(windows[1][:].indirect(slot_sb[:]), y_block_1[:])
-        nc.sync.dma_start(out[P:N, :], windows[1][:])
-        nc.vector.tensor_copy(windows[0][:].indirect(entries(slot_sb, HALF, S)), y_late[:])
+        for a, b in ((0, PIECE), (PIECE, S)):
+            nc.scalar.activation(windows[0][:].indirect(entries(slot_sb, a, b)), y[0][:, a:b], COPY)
         nc.sync.dma_start(out[0:P, :], windows[0][:])
+        nc.vector.tensor_copy(windows[1][:].indirect(slot_sb[:]), y[1][:])
+        nc.sync.dma_start(out[P:N, :], windows[1][:])

@@ -23,7 +23,9 @@ QUADRANT = 32
 SCALE_ROWS = 4
 ROW_ALIGN = 256
 PIECE = 128
-SCALAR_SHARE = (256, 320)
+LOAD_ORDER = (2, 0, 1, 3)
+HALF = S // 2
+LAST_SHARE = 320
 PIECES = ((0, 128), (128, 256), (256, 512))
 
 
@@ -53,12 +55,12 @@ def tile_picked_kvput_none_e_kernel(tc, xT, mem, w1_words, w1_scales, offs, slot
         w_rows = w1_words.rearrange("z p n r -> z p (n r)").bitcast(I32)
         planes = {}
         for z in range(PASSES):
-            for t in range(PACK):
+            for t in LOAD_ORDER:
                 planes[z, t] = keep.tile([P, T], F32, name="plane_%d_%d" % (z, t), align_bytes=ROW_ALIGN)
                 if (z, t) == (PASSES - 1, PACK - 1):
                     nc.sync.dma_start(w_words[0][:].bitcast(I32), w_rows[0])
                 nc.sync.dma_start(planes[z, t][:], x_rows[z, t])
-                if (z, t) == (0, 0):
+                if (z, t) == (0, LOAD_ORDER[0]):
                     nc.sync.dma_start(offs_sb[:], offs)
         windows = [keep.tile([P, U], F32, name="window_%d" % m, align_bytes=ROW_ALIGN) for m in range(ROW_BLOCKS)]
         nc.sync.dma_start(w_words[1][:].bitcast(I32), w_rows[1])
@@ -102,24 +104,25 @@ def tile_picked_kvput_none_e_kernel(tc, xT, mem, w1_words, w1_scales, offs, slot
                 stop=(z == PASSES - 1),
             )
 
-        for t in range(PACK):
-            gather_vector(0, t, SCALAR_SHARE[0], S)
-            gather_scalar(0, t, 0, SCALAR_SHARE[0])
+        for t in LOAD_ORDER:
+            gather_vector(0, t, HALF, S)
+            gather_scalar(0, t, 0, HALF)
         quantise(0, 0, S)
         for a, b in PIECES:
             for m in range(ROW_BLOCKS):
                 product(0, m, a, b)
-        for t in range(PACK - 1):
-            gather_vector(1, t, SCALAR_SHARE[1], S)
-            gather_scalar(1, t, 0, SCALAR_SHARE[1])
-        gather_vector(1, PACK - 1, SCALAR_SHARE[1], S)
-        for a in range(0, SCALAR_SHARE[1], PIECE):
-            gather_scalar(1, PACK - 1, a, min(a + PIECE, SCALAR_SHARE[1]))
+        for t in LOAD_ORDER[:-1]:
+            share = LAST_SHARE if t == 2 else HALF
+            gather_vector(1, t, share, S)
+            gather_scalar(1, t, 0, share)
+        gather_vector(1, PACK - 1, LAST_SHARE, S)
+        for a in range(0, LAST_SHARE, PIECE):
+            gather_scalar(1, PACK - 1, a, min(a + PIECE, LAST_SHARE))
 
         y = [keep.tile([P, S], F32, name="y_%d" % m) for m in range(ROW_BLOCKS)]
         for a, b in PIECES:
             quantise(1, a, b)
-            for m in range(ROW_BLOCKS):
+            for m in (0, 1) if a == 0 else (1, 0):
                 product(1, m, a, b)
                 if a == 0:
                     nc.scalar.copy(y[m][:, a:b], acc[m, a][:])

@@ -25,8 +25,8 @@ ROW_ALIGN = 256
 PIECE = 128
 LOAD_ORDER = (2, 0, 1, 3)
 HALF = S // 2
-LAST_SHARE = 320
-PIECES = ((0, 128), (128, 256), (256, 512))
+LAST_SHARE = 352
+PIECES = ((0, 128), (256, 512), (128, 256))
 
 
 def tile_picked_kvput_none_e_kernel(tc, xT, mem, w1_words, w1_scales, offs, slot, out):
@@ -57,7 +57,7 @@ def tile_picked_kvput_none_e_kernel(tc, xT, mem, w1_words, w1_scales, offs, slot
         for z in range(PASSES):
             for t in LOAD_ORDER:
                 planes[z, t] = keep.tile([P, T], F32, name="plane_%d_%d" % (z, t), align_bytes=ROW_ALIGN)
-                if (z, t) == (PASSES - 1, PACK - 1):
+                if (z, t) == (PASSES - 1, LOAD_ORDER[2]):
                     nc.sync.dma_start(w_words[0][:].bitcast(I32), w_rows[0])
                 nc.sync.dma_start(planes[z, t][:], x_rows[z, t])
                 if (z, t) == (0, LOAD_ORDER[0]):
@@ -108,6 +108,17 @@ def tile_picked_kvput_none_e_kernel(tc, xT, mem, w1_words, w1_scales, offs, slot
             gather_vector(0, t, HALF, S)
             gather_scalar(0, t, 0, HALF)
         quantise(0, 0, S)
+        warm = psum.tile([QUADRANT, S], F32, name="warm")
+        for n in (S, PIECE, PIECE):
+            nc.tensor.matmul_mx(
+                out=warm[:, 0:n],
+                lhsT=w_words[0][:, 0:QUADRANT].bitcast(FP8X4),
+                lhsT_scale=w_scales[:, 0, 0:QUADRANT],
+                rhs=codes[0][:, 0:n].bitcast(FP8X4),
+                rhs_scale=scales[0][:, 0:n],
+                start=True,
+                stop=True,
+            )
         for a, b in PIECES:
             for m in range(ROW_BLOCKS):
                 product(0, m, a, b)
@@ -116,13 +127,13 @@ def tile_picked_kvput_none_e_kernel(tc, xT, mem, w1_words, w1_scales, offs, slot
             gather_vector(1, t, share, S)
             gather_scalar(1, t, 0, share)
         gather_vector(1, PACK - 1, LAST_SHARE, S)
-        for a in range(0, LAST_SHARE, PIECE):
-            gather_scalar(1, PACK - 1, a, min(a + PIECE, LAST_SHARE))
+        for a, b in PIECES:
+            gather_scalar(1, PACK - 1, a, min(b, LAST_SHARE))
 
         y = [keep.tile([P, S], F32, name="y_%d" % m) for m in range(ROW_BLOCKS)]
         for a, b in PIECES:
             quantise(1, a, b)
-            for m in (0, 1) if a == 0 else (1, 0):
+            for m in range(ROW_BLOCKS):
                 product(1, m, a, b)
                 if a == 0:
                     nc.scalar.copy(y[m][:, a:b], acc[m, a][:])

@@ -41,7 +41,7 @@ def tile_picked_kvput_none_e_kernel(tc, xT, mem, w1_words, w1_scales, offs, slot
         w_scales = keep.tile([P, PASSES, N], U8, name="w_scales", align_bytes=ROW_ALIGN)
         staged = keep.tile([SCALE_ROWS, PASSES, P // QUADRANT, N // 4], I32, name="staged", align_bytes=ROW_ALIGN)
         nc.vector.memset(w_scales[:].bitcast(I32), 0)
-        nc.scalar.dma_start(
+        nc.sync.dma_start(
             staged[:].rearrange("i z q c -> i (z q) c"),
             w1_scales.bitcast(I32).rearrange("z (q i) c -> i (z q) c", i=SCALE_ROWS),
         )
@@ -108,17 +108,6 @@ def tile_picked_kvput_none_e_kernel(tc, xT, mem, w1_words, w1_scales, offs, slot
             gather_vector(0, t, HALF, S)
             gather_scalar(0, t, 0, HALF)
         quantise(0, 0, S)
-        warm = psum.tile([QUADRANT, S], F32, name="warm")
-        for n in (S, PIECE, PIECE):
-            nc.tensor.matmul_mx(
-                out=warm[:, 0:n],
-                lhsT=w_words[0][:, 0:QUADRANT].bitcast(FP8X4),
-                lhsT_scale=w_scales[:, 0, 0:QUADRANT],
-                rhs=codes[0][:, 0:n].bitcast(FP8X4),
-                rhs_scale=scales[0][:, 0:n],
-                start=True,
-                stop=True,
-            )
         for a, b in PIECES:
             for m in range(ROW_BLOCKS):
                 product(0, m, a, b)

@@ -37,11 +37,12 @@ def tile_picked_kvput_none_e_kernel(tc, xT, mem, w1_words, w1_scales, offs, slot
 
         offs_sb = keep.tile([P, S // LIST_ROWS], U16, name="offs_sb", align_bytes=ROW_ALIGN)
         slot_sb = keep.tile([P, S // LIST_ROWS], U16, name="slot_sb", align_bytes=ROW_ALIGN)
-        w_words = [keep.tile([P, N], U32, name="w_words_%d" % z, align_bytes=ROW_ALIGN) for z in range(PASSES)]
+        w_first = keep.tile([P, PASSES, P], U32, name="w_first", align_bytes=ROW_ALIGN)
+        w_second = [keep.tile([P, P], U32, name="w_second_%d" % z, align_bytes=ROW_ALIGN) for z in range(PASSES)]
         w_scales = keep.tile([P, PASSES, N], U8, name="w_scales", align_bytes=ROW_ALIGN)
         staged = keep.tile([SCALE_ROWS, PASSES, P // QUADRANT, N // 4], I32, name="staged", align_bytes=ROW_ALIGN)
         nc.vector.memset(w_scales[:].bitcast(I32), 0)
-        nc.sync.dma_start(
+        nc.scalar.dma_start(
             staged[:].rearrange("i z q c -> i (z q) c"),
             w1_scales.bitcast(I32).rearrange("z (q i) c -> i (z q) c", i=SCALE_ROWS),
         )
@@ -52,20 +53,21 @@ def tile_picked_kvput_none_e_kernel(tc, xT, mem, w1_words, w1_scales, offs, slot
             )
 
         x_rows = xT.rearrange("(z p t) c -> z t p c", z=PASSES, t=PACK)
-        w_rows = w1_words.rearrange("z p n r -> z p (n r)").bitcast(I32)
+        w_rows = w1_words.rearrange("z p n r -> p z (n r)").bitcast(I32)
         planes = {}
         for z in range(PASSES):
             for t in LOAD_ORDER:
                 planes[z, t] = keep.tile([P, T], F32, name="plane_%d_%d" % (z, t), align_bytes=ROW_ALIGN)
                 if (z, t) == (PASSES - 1, LOAD_ORDER[2]):
-                    nc.sync.dma_start(w_words[0][:].bitcast(I32), w_rows[0])
+                    nc.sync.dma_start(w_second[0][:].bitcast(I32), w_rows[:, 0, P:N])
                 nc.sync.dma_start(planes[z, t][:], x_rows[z, t])
                 if (z, t) == (0, LOAD_ORDER[0]):
                     nc.sync.dma_start(offs_sb[:], offs)
         windows = [keep.tile([P, U], F32, name="window_%d" % m, align_bytes=ROW_ALIGN) for m in range(ROW_BLOCKS)]
-        nc.sync.dma_start(w_words[1][:].bitcast(I32), w_rows[1])
+        nc.sync.dma_start(w_first[:].bitcast(I32), w_rows[:, :, 0:P])
         nc.sync.dma_start(windows[0][:], mem[0:P, :])
         nc.sync.dma_start(slot_sb[:], slot)
+        nc.sync.dma_start(w_second[1][:].bitcast(I32), w_rows[:, 1, P:N])
         nc.sync.dma_start(windows[1][:], mem[P:N, :])
 
         def entries(list_tile, a, b):
@@ -96,7 +98,7 @@ def tile_picked_kvput_none_e_kernel(tc, xT, mem, w1_words, w1_scales, offs, slot
         def product(z, m, a, b):
             nc.tensor.matmul_mx(
                 out=acc[m, a][:],
-                lhsT=w_words[z][:, m * P : (m + 1) * P].bitcast(FP8X4),
+                lhsT=(w_second[z][:] if m else w_first[:, z, :]).bitcast(FP8X4),
                 lhsT_scale=w_scales[:, z, m * P : (m + 1) * P],
                 rhs=codes[z][:, a:b].bitcast(FP8X4),
                 rhs_scale=scales[z][:, a:b],
@@ -109,8 +111,7 @@ def tile_picked_kvput_none_e_kernel(tc, xT, mem, w1_words, w1_scales, offs, slot
             gather_scalar(0, t, 0, HALF)
         quantise(0, 0, S)
         for a, b in PIECES:
-            for m in range(ROW_BLOCKS):
-                product(0, m, a, b)
+            product(0, 1, a, b)
         for t in LOAD_ORDER[:-1]:
             share = LAST_SHARE if t == 2 else HALF
             gather_vector(1, t, share, S)
@@ -122,9 +123,13 @@ def tile_picked_kvput_none_e_kernel(tc, xT, mem, w1_words, w1_scales, offs, slot
         y = [keep.tile([P, S], F32, name="y_%d" % m) for m in range(ROW_BLOCKS)]
         for a, b in PIECES:
             quantise(1, a, b)
-            for m in range(ROW_BLOCKS):
+        product(0, 0, *PIECES[0])
+        for m in range(ROW_BLOCKS):
+            for i, (a, b) in enumerate(PIECES):
+                if m == 0 and i + 1 < len(PIECES):
+                    product(0, 0, *PIECES[i + 1])
                 product(1, m, a, b)
-                if a == 0:
+                if (m, a) == (0, 0):
                     nc.scalar.copy(y[m][:, a:b], acc[m, a][:])
                 else:
                     nc.vector.tensor_copy(y[m][:, a:b], acc[m, a][:])

@@ -106,9 +106,16 @@ def tile_picked_kvput_none_e_kernel(tc, xT, mem, w1_words, w1_scales, offs, slot
                 stop=(z == PASSES - 1),
             )
 
+        paired = keep.tile([P, S * PACK], BF16, name="paired")
+        pair_slots = paired[:].rearrange("p (u c e) -> p u c e", u=2, e=2)
         for t in LOAD_ORDER:
-            gather_vector(0, t, HALF, S)
-            gather_scalar(0, t, 0, HALF)
+            window = planes[0, t][:]
+            nc.vector.tensor_copy(pair_slots[:, t // 2, HALF:S, t % 2], window.indirect(entries(offs_sb, HALF, S)))
+            nc.scalar.activation(pair_slots[:, t // 2, 0:HALF, t % 2], window.indirect(entries(offs_sb, 0, HALF)), COPY)
+        nc.vector.tensor_copy(
+            woven[0][:].bitcast(I32).rearrange("p (c u) -> p c u", u=2),
+            paired[:].bitcast(I32).rearrange("p (u c) -> p c u", u=2),
+        )
         quantise(0, 0, S)
         for a, b in PIECES:
             product(0, 1, a, b)

@@ -25,8 +25,7 @@ ROW_ALIGN = 256
 PIECE = 128
 LOAD_ORDER = (2, 0, 1, 3)
 HALF = S // 2
-LAST_SHARE = 352
-PIECES = ((0, 128), (256, 512), (128, 256))
+PIECES = (0, 256, 384, 128)
 
 
 def tile_picked_kvput_none_e_kernel(tc, xT, mem, w1_words, w1_scales, offs, slot, out):
@@ -37,37 +36,36 @@ def tile_picked_kvput_none_e_kernel(tc, xT, mem, w1_words, w1_scales, offs, slot
 
         offs_sb = keep.tile([P, S // LIST_ROWS], U16, name="offs_sb", align_bytes=ROW_ALIGN)
         slot_sb = keep.tile([P, S // LIST_ROWS], U16, name="slot_sb", align_bytes=ROW_ALIGN)
-        w_first = keep.tile([P, PASSES, P], U32, name="w_first", align_bytes=ROW_ALIGN)
-        w_second = [keep.tile([P, P], U32, name="w_second_%d" % z, align_bytes=ROW_ALIGN) for z in range(PASSES)]
+        w_early = [keep.tile([P, P], U32, name="w_early_%d" % m, align_bytes=ROW_ALIGN) for m in range(ROW_BLOCKS)]
+        w_late = keep.tile([P, N], U32, name="w_late", align_bytes=ROW_ALIGN)
         w_scales = keep.tile([P, PASSES, N], U8, name="w_scales", align_bytes=ROW_ALIGN)
         staged = keep.tile([SCALE_ROWS, PASSES, P // QUADRANT, N // 4], I32, name="staged", align_bytes=ROW_ALIGN)
-        nc.vector.memset(w_scales[:].bitcast(I32), 0)
+        nc.vector.memset(w_scales[:, 1, :].bitcast(I32), 0)
+        nc.scalar.copy(w_scales[:, 0, :].bitcast(U32), w_scales[:, 1, :].bitcast(U32))
         nc.scalar.dma_start(
             staged[:].rearrange("i z q c -> i (z q) c"),
             w1_scales.bitcast(I32).rearrange("z (q i) c -> i (z q) c", i=SCALE_ROWS),
         )
-        nc.scalar.copy(w_scales[:].bitcast(U32)[0:SCALE_ROWS], staged[:, :, 0, :].bitcast(U32))
-        for q in range(1, P // QUADRANT):
+        for q in range(P // QUADRANT):
             nc.vector.tensor_copy(
                 w_scales[:].bitcast(I32)[q * QUADRANT : q * QUADRANT + SCALE_ROWS], staged[:, :, q, :]
             )
 
         x_rows = xT.rearrange("(z p t) c -> z t p c", z=PASSES, t=PACK)
-        w_rows = w1_words.rearrange("z p n r -> p z (n r)").bitcast(I32)
+        w_rows = w1_words.rearrange("z p n r -> z p (n r)").bitcast(I32)
         planes = {}
         for z in range(PASSES):
             for t in LOAD_ORDER:
                 planes[z, t] = keep.tile([P, T], F32, name="plane_%d_%d" % (z, t), align_bytes=ROW_ALIGN)
-                if (z, t) == (PASSES - 1, LOAD_ORDER[2]):
-                    nc.sync.dma_start(w_second[0][:].bitcast(I32), w_rows[:, 0, P:N])
                 nc.sync.dma_start(planes[z, t][:], x_rows[z, t])
                 if (z, t) == (0, LOAD_ORDER[0]):
                     nc.sync.dma_start(offs_sb[:], offs)
         windows = [keep.tile([P, U], F32, name="window_%d" % m, align_bytes=ROW_ALIGN) for m in range(ROW_BLOCKS)]
-        nc.sync.dma_start(w_first[:].bitcast(I32), w_rows[:, :, 0:P])
+        for m in range(ROW_BLOCKS):
+            nc.sync.dma_start(w_early[m][:].bitcast(I32), w_rows[0][:, m * P : (m + 1) * P])
+        nc.sync.dma_start(w_late[:].bitcast(I32), w_rows[1])
         nc.sync.dma_start(windows[0][:], mem[0:P, :])
         nc.sync.dma_start(slot_sb[:], slot)
-        nc.sync.dma_start(w_second[1][:].bitcast(I32), w_rows[:, 1, P:N])
         nc.sync.dma_start(windows[1][:], mem[P:N, :])
 
         def entries(list_tile, a, b):
@@ -91,14 +89,13 @@ def tile_picked_kvput_none_e_kernel(tc, xT, mem, w1_words, w1_scales, offs, slot
                 out=codes[z][:, a:b].bitcast(FP8X4), scales=scales[z][:, a:b], in_=woven[z][:, a * PACK : b * PACK]
             )
 
-        acc = {
-            (m, a): psum.tile([P, b - a], F32, name="acc_%d_%d" % (m, a)) for a, b in PIECES for m in range(ROW_BLOCKS)
-        }
+        acc = {(0, a): psum.tile([P, PIECE], F32, name="acc_0_%d" % a, tag="bank_%d" % a) for a in PIECES}
+        acc[1, HALF] = psum.tile([P, HALF], F32, name="acc_1_late_half")
 
         def product(z, m, a, b):
             nc.tensor.matmul_mx(
                 out=acc[m, a][:],
-                lhsT=(w_second[z][:] if m else w_first[:, z, :]).bitcast(FP8X4),
+                lhsT=(w_late[:, m * P : (m + 1) * P] if z else w_early[m][:]).bitcast(FP8X4),
                 lhsT_scale=w_scales[:, z, m * P : (m + 1) * P],
                 rhs=codes[z][:, a:b].bitcast(FP8X4),
                 rhs_scale=scales[z][:, a:b],
@@ -106,40 +103,38 @@ def tile_picked_kvput_none_e_kernel(tc, xT, mem, w1_words, w1_scales, offs, slot
                 stop=(z == PASSES - 1),
             )
 
-        paired = keep.tile([P, S * PACK], BF16, name="paired")
-        pair_slots = paired[:].rearrange("p (u c e) -> p u c e", u=2, e=2)
         for t in LOAD_ORDER:
-            window = planes[0, t][:]
-            nc.vector.tensor_copy(pair_slots[:, t // 2, HALF:S, t % 2], window.indirect(entries(offs_sb, HALF, S)))
-            nc.scalar.activation(pair_slots[:, t // 2, 0:HALF, t % 2], window.indirect(entries(offs_sb, 0, HALF)), COPY)
-        nc.vector.tensor_copy(
-            woven[0][:].bitcast(I32).rearrange("p (c u) -> p c u", u=2),
-            paired[:].bitcast(I32).rearrange("p (u c) -> p c u", u=2),
-        )
+            gather_vector(0, t, 0, HALF)
+            gather_scalar(0, t, HALF, S)
         quantise(0, 0, S)
-        for a, b in PIECES:
-            product(0, 1, a, b)
+        for a in PIECES:
+            product(0, 0, a, a + PIECE)
+        product(0, 1, HALF, S)
         for t in LOAD_ORDER[:-1]:
-            share = LAST_SHARE if t == 2 else HALF
-            gather_vector(1, t, share, S)
-            gather_scalar(1, t, 0, share)
-        gather_vector(1, PACK - 1, LAST_SHARE, S)
-        for a, b in PIECES:
-            gather_scalar(1, PACK - 1, a, min(b, LAST_SHARE))
+            share = PIECE if t == 2 else HALF
+            gather_vector(1, t, 0, share)
+            gather_scalar(1, t, share, S)
+        gather_vector(1, PACK - 1, 0, PIECE)
+        for a in PIECES[1:]:
+            gather_scalar(1, PACK - 1, a, a + PIECE)
 
         y = [keep.tile([P, S], F32, name="y_%d" % m) for m in range(ROW_BLOCKS)]
-        for a, b in PIECES:
-            quantise(1, a, b)
-        product(0, 0, *PIECES[0])
-        for m in range(ROW_BLOCKS):
-            for i, (a, b) in enumerate(PIECES):
-                if m == 0 and i + 1 < len(PIECES):
-                    product(0, 0, *PIECES[i + 1])
-                product(1, m, a, b)
-                if (m, a) == (0, 0):
-                    nc.scalar.copy(y[m][:, a:b], acc[m, a][:])
-                else:
-                    nc.vector.tensor_copy(y[m][:, a:b], acc[m, a][:])
+        for a in PIECES:
+            quantise(1, a, a + PIECE)
+        for a in PIECES:
+            if a == PIECES[-1]:
+                product(1, 1, HALF, S)
+            product(1, 0, a, a + PIECE)
+        nc.scalar.copy(y[0][:, 0:PIECE], acc[0, 0][:])
+        for a in PIECES[1:]:
+            if a == PIECES[-1]:
+                nc.vector.tensor_copy(y[1][:, HALF:S], acc[1, HALF][:])
+            nc.vector.tensor_copy(y[0][:, a : a + PIECE], acc[0, a][:])
+        for a, bank in zip((0, PIECE), PIECES):
+            acc[1, a] = psum.tile([P, PIECE], F32, name="acc_1_%d" % a, tag="bank_%d" % bank)
+            for z in range(PASSES):
+                product(z, 1, a, a + PIECE)
+            nc.vector.tensor_copy(y[1][:, a : a + PIECE], acc[1, a][:])
 
         for a, b in ((0, PIECE), (PIECE, S)):
             nc.scalar.activation(windows[0][:].indirect(entries(slot_sb, a, b)), y[0][:, a:b], COPY)

@@ -89,27 +89,30 @@ def tile_picked_kvput_none_e_kernel(tc, xT, mem, w1_words, w1_scales, offs, slot
                 out=codes[z][:, a:b].bitcast(FP8X4), scales=scales[z][:, a:b], in_=woven[z][:, a * PACK : b * PACK]
             )
 
-        acc = {(0, a): psum.tile([P, PIECE], F32, name="acc_0_%d" % a, tag="bank_%d" % a) for a in PIECES}
-        acc[1, HALF] = psum.tile([P, HALF], F32, name="acc_1_late_half")
+        acc = {}
+        for m in range(ROW_BLOCKS):
+            acc[m, 0] = psum.tile([P, PIECE], F32, name="acc_%d_first" % m, tag="bank_%d" % m)[:]
+            acc[m, HALF] = psum.tile([P, HALF], F32, name="acc_%d_half" % m)[:]
 
-        def product(z, m, a, b):
+        def product(z, m, a, b, group=None):
+            first, last = group or (a, b)
             nc.tensor.matmul_mx(
-                out=acc[m, a][:],
+                out=acc[m, first][:, a - first : b - first],
                 lhsT=(w_late[:, m * P : (m + 1) * P] if z else w_early[m][:]).bitcast(FP8X4),
                 lhsT_scale=w_scales[:, z, m * P : (m + 1) * P],
                 rhs=codes[z][:, a:b].bitcast(FP8X4),
                 rhs_scale=scales[z][:, a:b],
                 start=(z == 0),
-                stop=(z == PASSES - 1),
+                stop=(z == PASSES - 1 and b == last),
             )
 
         for t in LOAD_ORDER:
             gather_vector(0, t, 0, HALF)
             gather_scalar(0, t, HALF, S)
         quantise(0, 0, S)
-        for a in PIECES:
-            product(0, 0, a, a + PIECE)
-        product(0, 1, HALF, S)
+        for m in range(ROW_BLOCKS):
+            product(0, m, 0, PIECE)
+            product(0, m, HALF, S)
         for t in LOAD_ORDER[:-1]:
             share = PIECE if t == 2 else HALF
             gather_vector(1, t, 0, share)
@@ -121,20 +124,20 @@ def tile_picked_kvput_none_e_kernel(tc, xT, mem, w1_words, w1_scales, offs, slot
         y = [keep.tile([P, S], F32, name="y_%d" % m) for m in range(ROW_BLOCKS)]
         for a in PIECES:
             quantise(1, a, a + PIECE)
-        for a in PIECES:
-            if a == PIECES[-1]:
-                product(1, 1, HALF, S)
-            product(1, 0, a, a + PIECE)
-        nc.scalar.copy(y[0][:, 0:PIECE], acc[0, 0][:])
-        for a in PIECES[1:]:
-            if a == PIECES[-1]:
-                nc.vector.tensor_copy(y[1][:, HALF:S], acc[1, HALF][:])
-            nc.vector.tensor_copy(y[0][:, a : a + PIECE], acc[0, a][:])
-        for a, bank in zip((0, PIECE), PIECES):
-            acc[1, a] = psum.tile([P, PIECE], F32, name="acc_1_%d" % a, tag="bank_%d" % bank)
+        for m in range(ROW_BLOCKS):
+            product(1, m, 0, PIECE)
+        for a in PIECES[1:-1]:
+            product(1, 0, a, a + PIECE, (HALF, S))
+        product(1, 1, HALF, S)
+        nc.scalar.copy(y[0][:, 0:PIECE], acc[0, 0])
+        nc.vector.tensor_copy(y[1][:, 0:PIECE], acc[1, 0])
+        for m in range(ROW_BLOCKS):
+            nc.vector.tensor_copy(y[m][:, HALF:S], acc[m, HALF])
+        for m in range(ROW_BLOCKS):
+            acc[m, PIECE] = psum.tile([P, PIECE], F32, name="acc_%d_last" % m, tag="bank_%d" % m)[:]
             for z in range(PASSES):
-                product(z, 1, a, a + PIECE)
-            nc.vector.tensor_copy(y[1][:, a : a + PIECE], acc[1, a][:])
+                product(z, m, PIECE, HALF)
+            nc.vector.tensor_copy(y[m][:, PIECE:HALF], acc[m, PIECE])
 
         for a, b in ((0, PIECE), (PIECE, S)):
             nc.scalar.activation(windows[0][:].indirect(entries(slot_sb, a, b)), y[0][:, a:b], COPY)

@@ -39,17 +39,11 @@ def tile_picked_kvput_none_e_kernel(tc, xT, mem, w1_words, w1_scales, offs, slot
         w_early = [keep.tile([P, P], U32, name="w_early_%d" % m, align_bytes=ROW_ALIGN) for m in range(ROW_BLOCKS)]
         w_late = keep.tile([P, N], U32, name="w_late", align_bytes=ROW_ALIGN)
         w_scales = keep.tile([P, PASSES, N], U8, name="w_scales", align_bytes=ROW_ALIGN)
-        staged = keep.tile([SCALE_ROWS, PASSES, P // QUADRANT, N // 4], I32, name="staged", align_bytes=ROW_ALIGN)
         nc.vector.memset(w_scales[:, 1, :].bitcast(I32), 0)
         nc.scalar.copy(w_scales[:, 0, :].bitcast(U32), w_scales[:, 1, :].bitcast(U32))
-        nc.scalar.dma_start(
-            staged[:].rearrange("i z q c -> i (z q) c"),
-            w1_scales.bitcast(I32).rearrange("z (q i) c -> i (z q) c", i=SCALE_ROWS),
-        )
-        for q in range(P // QUADRANT):
-            nc.vector.tensor_copy(
-                w_scales[:].bitcast(I32)[q * QUADRANT : q * QUADRANT + SCALE_ROWS], staged[:, :, q, :]
-            )
+        scale_rows = w1_scales.bitcast(I32).rearrange("z (q i) c -> i q z c", i=SCALE_ROWS)
+        for i in range(SCALE_ROWS):
+            nc.scalar.dma_start(w_scales[:].bitcast(I32)[i:P:QUADRANT], scale_rows[i])
 
         x_rows = xT.rearrange("(z p t) c -> z t p c", z=PASSES, t=PACK)
         w_rows = w1_words.rearrange("z p n r -> z p (n r)").bitcast(I32)
@@ -92,18 +86,19 @@ def tile_picked_kvput_none_e_kernel(tc, xT, mem, w1_words, w1_scales, offs, slot
         acc = {}
         for m in range(ROW_BLOCKS):
             acc[m, 0] = psum.tile([P, PIECE], F32, name="acc_%d_first" % m, tag="bank_%d" % m)[:]
-            acc[m, HALF] = psum.tile([P, HALF], F32, name="acc_%d_half" % m)[:]
+            for a in PIECES[1:-1]:
+                acc[m, a] = psum.tile([P, PIECE], F32, name="acc_%d_%d" % (m, a))[:]
 
-        def product(z, m, a, b, group=None):
-            first, last = group or (a, b)
+        def product(z, m, a):
+            b = a + PIECE
             nc.tensor.matmul_mx(
-                out=acc[m, first][:, a - first : b - first],
+                out=acc[m, a],
                 lhsT=(w_late[:, m * P : (m + 1) * P] if z else w_early[m][:]).bitcast(FP8X4),
                 lhsT_scale=w_scales[:, z, m * P : (m + 1) * P],
                 rhs=codes[z][:, a:b].bitcast(FP8X4),
                 rhs_scale=scales[z][:, a:b],
                 start=(z == 0),
-                stop=(z == PASSES - 1 and b == last),
+                stop=(z == PASSES - 1),
             )
 
         for t in LOAD_ORDER:
@@ -111,8 +106,8 @@ def tile_picked_kvput_none_e_kernel(tc, xT, mem, w1_words, w1_scales, offs, slot
             gather_scalar(0, t, HALF, S)
         quantise(0, 0, S)
         for m in range(ROW_BLOCKS):
-            product(0, m, 0, PIECE)
-            product(0, m, HALF, S)
+            for a in PIECES[:-1]:
+                product(0, m, a)
         for t in LOAD_ORDER[:-1]:
             share = PIECE if t == 2 else HALF
             gather_vector(1, t, 0, share)
@@ -124,19 +119,17 @@ def tile_picked_kvput_none_e_kernel(tc, xT, mem, w1_words, w1_scales, offs, slot
         y = [keep.tile([P, S], F32, name="y_%d" % m) for m in range(ROW_BLOCKS)]
         for a in PIECES:
             quantise(1, a, a + PIECE)
-        for m in range(ROW_BLOCKS):
-            product(1, m, 0, PIECE)
-        for a in PIECES[1:-1]:
-            product(1, 0, a, a + PIECE, (HALF, S))
-        product(1, 1, HALF, S)
-        nc.scalar.copy(y[0][:, 0:PIECE], acc[0, 0])
-        nc.vector.tensor_copy(y[1][:, 0:PIECE], acc[1, 0])
-        for m in range(ROW_BLOCKS):
-            nc.vector.tensor_copy(y[m][:, HALF:S], acc[m, HALF])
+        for a in PIECES[:-1]:
+            for m in range(ROW_BLOCKS):
+                product(1, m, a)
+                if (m, a) == (0, 0):
+                    nc.scalar.copy(y[m][:, a : a + PIECE], acc[m, a])
+                else:
+                    nc.vector.tensor_copy(y[m][:, a : a + PIECE], acc[m, a])
         for m in range(ROW_BLOCKS):
             acc[m, PIECE] = psum.tile([P, PIECE], F32, name="acc_%d_last" % m, tag="bank_%d" % m)[:]
             for z in range(PASSES):
-                product(z, m, PIECE, HALF)
+                product(z, m, PIECE)
             nc.vector.tensor_copy(y[m][:, PIECE:HALF], acc[m, PIECE])
 
         for a, b in ((0, PIECE), (PIECE, S)):

@@ -25,7 +25,6 @@ ROW_ALIGN = 256
 PIECE = 128
 LOAD_ORDER = (2, 0, 1, 3)
 HALF = S // 2
-PIECES = (0, 256, 384, 128)
 
 
 def tile_picked_kvput_none_e_kernel(tc, xT, mem, w1_words, w1_scales, offs, slot, out):
@@ -83,22 +82,21 @@ def tile_picked_kvput_none_e_kernel(tc, xT, mem, w1_words, w1_scales, offs, slot
                 out=codes[z][:, a:b].bitcast(FP8X4), scales=scales[z][:, a:b], in_=woven[z][:, a * PACK : b * PACK]
             )
 
+        first, middle, last = (0, PIECE), (PIECE, S - PIECE), (S - PIECE, S)
         acc = {}
         for m in range(ROW_BLOCKS):
-            acc[m, 0] = psum.tile([P, PIECE], F32, name="acc_%d_first" % m, tag="bank_%d" % m)[:]
-            for a in PIECES[1:-1]:
-                acc[m, a] = psum.tile([P, PIECE], F32, name="acc_%d_%d" % (m, a))[:]
+            acc[m, first] = psum.tile([P, PIECE], F32, name="acc_%d_first" % m, tag="bank_%d" % m)
+            acc[m, middle] = psum.tile([P, HALF], F32, name="acc_%d_middle" % m)
 
-        def product(z, m, a):
-            b = a + PIECE
+        def product(z, m, group, a, b):
             nc.tensor.matmul_mx(
-                out=acc[m, a],
+                out=acc[m, group][:, a - group[0] : b - group[0]],
                 lhsT=(w_late[:, m * P : (m + 1) * P] if z else w_early[m][:]).bitcast(FP8X4),
                 lhsT_scale=w_scales[:, z, m * P : (m + 1) * P],
                 rhs=codes[z][:, a:b].bitcast(FP8X4),
                 rhs_scale=scales[z][:, a:b],
                 start=(z == 0),
-                stop=(z == PASSES - 1),
+                stop=(z == PASSES - 1 and b == group[1]),
             )
 
         for t in LOAD_ORDER:
@@ -106,34 +104,34 @@ def tile_picked_kvput_none_e_kernel(tc, xT, mem, w1_words, w1_scales, offs, slot
             gather_scalar(0, t, HALF, S)
         quantise(0, 0, S)
         for m in range(ROW_BLOCKS):
-            for a in PIECES[:-1]:
-                product(0, m, a)
+            for group in (first, middle):
+                product(0, m, group, *group)
         for t in LOAD_ORDER[:-1]:
             share = PIECE if t == 2 else HALF
             gather_vector(1, t, 0, share)
             gather_scalar(1, t, share, S)
         gather_vector(1, PACK - 1, 0, PIECE)
-        for a in PIECES[1:]:
+        for a in range(PIECE, S, PIECE):
             gather_scalar(1, PACK - 1, a, a + PIECE)
 
         y = [keep.tile([P, S], F32, name="y_%d" % m) for m in range(ROW_BLOCKS)]
-        for a in PIECES:
+        for a in range(0, S, PIECE):
             quantise(1, a, a + PIECE)
-        for a in PIECES[:-1]:
+        for group in (first, middle):
+            for a in range(group[0], group[1], PIECE):
+                for m in range(ROW_BLOCKS):
+                    product(1, m, group, a, a + PIECE)
             for m in range(ROW_BLOCKS):
-                product(1, m, a)
-                if (m, a) == (0, 0):
-                    nc.scalar.copy(y[m][:, a : a + PIECE], acc[m, a])
-                else:
-                    nc.vector.tensor_copy(y[m][:, a : a + PIECE], acc[m, a])
+                nc.scalar.copy(y[m][:, group[0] : group[1]], acc[m, group][:])
         for m in range(ROW_BLOCKS):
-            acc[m, PIECE] = psum.tile([P, PIECE], F32, name="acc_%d_last" % m, tag="bank_%d" % m)[:]
+            acc[m, last] = psum.tile([P, PIECE], F32, name="acc_%d_last" % m, tag="bank_%d" % m)
             for z in range(PASSES):
-                product(z, m, PIECE)
-            nc.vector.tensor_copy(y[m][:, PIECE:HALF], acc[m, PIECE])
+                product(z, m, last, *last)
+            nc.scalar.copy(y[m][:, last[0] : last[1]], acc[m, last][:])
 
         for a, b in ((0, PIECE), (PIECE, S)):
-            nc.scalar.activation(windows[0][:].indirect(entries(slot_sb, a, b)), y[0][:, a:b], COPY)
+            nc.vector.tensor_copy(windows[0][:].indirect(entries(slot_sb, a, b)), y[0][:, a:b])
         nc.sync.dma_start(out[0:P, :], windows[0][:])
-        nc.vector.tensor_copy(windows[1][:].indirect(slot_sb[:]), y[1][:])
+        for a, b in ((0, HALF), (HALF, S)):
+            nc.scalar.activation(windows[1][:].indirect(entries(slot_sb, a, b)), y[1][:, a:b], COPY)
         nc.sync.dma_start(out[P:N, :], windows[1][:])

@@ -49,13 +49,14 @@ def tile_picked_kvput_none_e_kernel(tc, xT, mem, w1_words, w1_scales, offs, slot
         planes = {}
         for z in range(PASSES):
             for t in LOAD_ORDER:
+                if (z, t) == (PASSES - 1, LOAD_ORDER[-1]):
+                    nc.sync.dma_start(w_early[0][:].bitcast(I32), w_rows[0][:, 0:P])
                 planes[z, t] = keep.tile([P, T], F32, name="plane_%d_%d" % (z, t), align_bytes=ROW_ALIGN)
                 nc.sync.dma_start(planes[z, t][:], x_rows[z, t])
                 if (z, t) == (0, LOAD_ORDER[0]):
                     nc.sync.dma_start(offs_sb[:], offs)
         windows = [keep.tile([P, U], F32, name="window_%d" % m, align_bytes=ROW_ALIGN) for m in range(ROW_BLOCKS)]
-        for m in range(ROW_BLOCKS):
-            nc.sync.dma_start(w_early[m][:].bitcast(I32), w_rows[0][:, m * P : (m + 1) * P])
+        nc.sync.dma_start(w_early[1][:].bitcast(I32), w_rows[0][:, P:N])
         nc.sync.dma_start(w_late[:].bitcast(I32), w_rows[1])
         nc.sync.dma_start(windows[0][:], mem[0:P, :])
         nc.sync.dma_start(slot_sb[:], slot)
@@ -82,11 +83,11 @@ def tile_picked_kvput_none_e_kernel(tc, xT, mem, w1_words, w1_scales, offs, slot
                 out=codes[z][:, a:b].bitcast(FP8X4), scales=scales[z][:, a:b], in_=woven[z][:, a * PACK : b * PACK]
             )
 
-        first, middle, last = (0, PIECE), (PIECE, S - PIECE), (S - PIECE, S)
+        groups = ((0, PIECE), (PIECE, S - PIECE), (S - PIECE, S))
         acc = {}
         for m in range(ROW_BLOCKS):
-            acc[m, first] = psum.tile([P, PIECE], F32, name="acc_%d_first" % m, tag="bank_%d" % m)
-            acc[m, middle] = psum.tile([P, HALF], F32, name="acc_%d_middle" % m)
+            for a, b in groups:
+                acc[m, (a, b)] = psum.tile([P, b - a], F32, name="acc_%d_%d" % (m, a))
 
         def product(z, m, group, a, b):
             nc.tensor.matmul_mx(
@@ -104,7 +105,7 @@ def tile_picked_kvput_none_e_kernel(tc, xT, mem, w1_words, w1_scales, offs, slot
             gather_scalar(0, t, HALF, S)
         quantise(0, 0, S)
         for m in range(ROW_BLOCKS):
-            for group in (first, middle):
+            for group in groups:
                 product(0, m, group, *group)
         for t in LOAD_ORDER[:-1]:
             share = PIECE if t == 2 else HALF
@@ -117,17 +118,12 @@ def tile_picked_kvput_none_e_kernel(tc, xT, mem, w1_words, w1_scales, offs, slot
         y = [keep.tile([P, S], F32, name="y_%d" % m) for m in range(ROW_BLOCKS)]
         for a in range(0, S, PIECE):
             quantise(1, a, a + PIECE)
-        for group in (first, middle):
+        for group in groups:
             for a in range(group[0], group[1], PIECE):
                 for m in range(ROW_BLOCKS):
                     product(1, m, group, a, a + PIECE)
             for m in range(ROW_BLOCKS):
                 nc.scalar.copy(y[m][:, group[0] : group[1]], acc[m, group][:])
-        for m in range(ROW_BLOCKS):
-            acc[m, last] = psum.tile([P, PIECE], F32, name="acc_%d_last" % m, tag="bank_%d" % m)
-            for z in range(PASSES):
-                product(z, m, last, *last)
-            nc.scalar.copy(y[m][:, last[0] : last[1]], acc[m, last][:])
 
         for a, b in ((0, PIECE), (PIECE, S)):
             nc.vector.tensor_copy(windows[0][:].indirect(entries(slot_sb, a, b)), y[0][:, a:b])

@@ -83,7 +83,7 @@ def tile_picked_kvput_none_e_kernel(tc, xT, mem, w1_words, w1_scales, offs, slot
                 out=codes[z][:, a:b].bitcast(FP8X4), scales=scales[z][:, a:b], in_=woven[z][:, a * PACK : b * PACK]
             )
 
-        groups = ((0, PIECE), (PIECE, S - PIECE), (S - PIECE, S))
+        groups = [(a, a + PIECE) for a in range(0, S, PIECE)]
         acc = {}
         for m in range(ROW_BLOCKS):
             for a, b in groups:
@@ -119,15 +119,15 @@ def tile_picked_kvput_none_e_kernel(tc, xT, mem, w1_words, w1_scales, offs, slot
         for a in range(0, S, PIECE):
             quantise(1, a, a + PIECE)
         for group in groups:
-            for a in range(group[0], group[1], PIECE):
-                for m in range(ROW_BLOCKS):
-                    product(1, m, group, a, a + PIECE)
             for m in range(ROW_BLOCKS):
-                nc.scalar.copy(y[m][:, group[0] : group[1]], acc[m, group][:])
+                product(1, m, group, *group)
+                if (m, group[0]) == (0, 0):
+                    nc.scalar.copy(y[m][:, group[0] : group[1]], acc[m, group][:])
+                else:
+                    nc.vector.tensor_copy(y[m][:, group[0] : group[1]], acc[m, group][:])
 
         for a, b in ((0, PIECE), (PIECE, S)):
-            nc.vector.tensor_copy(windows[0][:].indirect(entries(slot_sb, a, b)), y[0][:, a:b])
+            nc.scalar.activation(windows[0][:].indirect(entries(slot_sb, a, b)), y[0][:, a:b], COPY)
         nc.sync.dma_start(out[0:P, :], windows[0][:])
-        for a, b in ((0, HALF), (HALF, S)):
-            nc.scalar.activation(windows[1][:].indirect(entries(slot_sb, a, b)), y[1][:, a:b], COPY)
+        nc.vector.tensor_copy(windows[1][:].indirect(slot_sb[:]), y[1][:])
         nc.sync.dma_start(out[P:N, :], windows[1][:])

from contextlib import ExitStack

import concourse.mybir as mybir

K, T, S, N, U = 1024, 1024, 512, 256, 1024
FLOPS = 2 * K * S * N

F32 = mybir.dt.float32
BF16 = mybir.dt.bfloat16
I32 = mybir.dt.int32
U32 = mybir.dt.uint32
U16 = mybir.dt.uint16
U8 = mybir.dt.uint8
COPY = mybir.ActivationFunctionType.Copy
FP8X4 = mybir.dt.float8_e4m3fn_x4

P = 128
PACK = 4
PASSES = K // (P * PACK)
ROW_BLOCKS = N // P
LIST_ROWS = 16
QUADRANT = 32
SCALE_ROWS = 4
ROW_ALIGN = 256
PIECE = 128
LOAD_ORDER = (2, 0, 1, 3)
HALF = S // 2


def tile_picked_kvput_none_e_kernel(tc, xT, mem, w1_words, w1_scales, offs, slot, out):
    nc = tc.nc
    with ExitStack() as ctx:
        keep = ctx.enter_context(tc.tile_pool(name="keep", bufs=1))
        psum = ctx.enter_context(tc.psum_pool(name="psum", bufs=1))

        offs_sb = keep.tile([P, S // LIST_ROWS], U16, name="offs_sb", align_bytes=ROW_ALIGN)
        slot_sb = keep.tile([P, S // LIST_ROWS], U16, name="slot_sb", align_bytes=ROW_ALIGN)
        w_early = [keep.tile([P, P], U32, name="w_early_%d" % m, align_bytes=ROW_ALIGN) for m in range(ROW_BLOCKS)]
        w_late = keep.tile([P, N], U32, name="w_late", align_bytes=ROW_ALIGN)
        w_scales = keep.tile([P, PASSES, N], U8, name="w_scales", align_bytes=ROW_ALIGN)
        nc.vector.memset(w_scales[:, 1, :].bitcast(I32), 0)
        nc.scalar.copy(w_scales[:, 0, :].bitcast(U32), w_scales[:, 1, :].bitcast(U32))
        scale_rows = w1_scales.bitcast(I32).rearrange("z (q i) c -> i q z c", i=SCALE_ROWS)
        for i in range(SCALE_ROWS):
            nc.scalar.dma_start(w_scales[:].bitcast(I32)[i:P:QUADRANT], scale_rows[i])

        x_rows = xT.rearrange("(z p t) c -> z t p c", z=PASSES, t=PACK)
        w_rows = w1_words.rearrange("z p n r -> z p (n r)").bitcast(I32)
        planes = {}
        for z in range(PASSES):
            for t in LOAD_ORDER:
                if (z, t) == (PASSES - 1, LOAD_ORDER[-1]):
                    nc.sync.dma_start(w_early[0][:].bitcast(I32), w_rows[0][:, 0:P])
                planes[z, t] = keep.tile([P, T], F32, name="plane_%d_%d" % (z, t), align_bytes=ROW_ALIGN)
                nc.sync.dma_start(planes[z, t][:], x_rows[z, t])
                if (z, t) == (0, LOAD_ORDER[0]):
                    nc.sync.dma_start(offs_sb[:], offs)
        windows = [keep.tile([P, U], F32, name="window_%d" % m, align_bytes=ROW_ALIGN) for m in range(ROW_BLOCKS)]
        nc.sync.dma_start(w_early[1][:].bitcast(I32), w_rows[0][:, P:N])
        nc.sync.dma_start(w_late[:].bitcast(I32), w_rows[1])
        nc.sync.dma_start(windows[0][:], mem[0:P, :])
        nc.sync.dma_start(slot_sb[:], slot)
        nc.sync.dma_start(windows[1][:], mem[P:N, :])

        def entries(list_tile, a, b):
            return list_tile[:, a // LIST_ROWS : b // LIST_ROWS]

        woven = [keep.tile([P, S * PACK], BF16, name="woven_%d" % z, align_bytes=64) for z in range(PASSES)]
        codes = [keep.tile([P, S], U32, name="codes_%d" % z, align_bytes=64) for z in range(PASSES)]
        scales = [keep.tile([P, S], U8, name="scales_%d" % z, align_bytes=64) for z in range(PASSES)]

        def picked(z, t, a, b):
            return woven[z][:, a * PACK + t : b * PACK : PACK], planes[z, t][:].indirect(entries(offs_sb, a, b))

        def gather_vector(z, t, a, b):
            nc.vector.tensor_copy(*picked(z, t, a, b))

        def gather_scalar(z, t, a, b):
            nc.scalar.activation(*picked(z, t, a, b), COPY)

        def quantise(z, a, b):
            nc.vector.quantize_mx(
                out=codes[z][:, a:b].bitcast(FP8X4), scales=scales[z][:, a:b], in_=woven[z][:, a * PACK : b * PACK]
            )

        groups = [(a, a + PIECE) for a in range(0, S, PIECE)]
        acc = {}
        for m in range(ROW_BLOCKS):
            for a, b in groups:
                acc[m, (a, b)] = psum.tile([P, b - a], F32, name="acc_%d_%d" % (m, a))

        def product(z, m, group, a, b):
            nc.tensor.matmul_mx(
                out=acc[m, group][:, a - group[0] : b - group[0]],
                lhsT=(w_late[:, m * P : (m + 1) * P] if z else w_early[m][:]).bitcast(FP8X4),
                lhsT_scale=w_scales[:, z, m * P : (m + 1) * P],
                rhs=codes[z][:, a:b].bitcast(FP8X4),
                rhs_scale=scales[z][:, a:b],
                start=(z == 0),
                stop=(z == PASSES - 1 and b == group[1]),
            )

        for t in LOAD_ORDER:
            gather_vector(0, t, 0, HALF)
            gather_scalar(0, t, HALF, S)
        quantise(0, 0, S)
        for m in range(ROW_BLOCKS):
            for group in groups:
                product(0, m, group, *group)
        for t in LOAD_ORDER[:-1]:
            share = PIECE if t == 2 else HALF
            gather_vector(1, t, 0, share)
            gather_scalar(1, t, share, S)
        gather_vector(1, PACK - 1, 0, PIECE)
        for a in range(PIECE, S, PIECE):
            gather_scalar(1, PACK - 1, a, a + PIECE)

        y = [keep.tile([P, S], F32, name="y_%d" % m) for m in range(ROW_BLOCKS)]
        for a in range(0, S, PIECE):
            quantise(1, a, a + PIECE)
        for group in groups:
            for m in range(ROW_BLOCKS):
                product(1, m, group, *group)
                if (m, group[0]) == (0, 0):
                    nc.scalar.copy(y[m][:, group[0] : group[1]], acc[m, group][:])
                else:
                    nc.vector.tensor_copy(y[m][:, group[0] : group[1]], acc[m, group][:])

        for a, b in ((0, PIECE), (PIECE, S)):
            nc.scalar.activation(windows[0][:].indirect(entries(slot_sb, a, b)), y[0][:, a:b], COPY)
        nc.sync.dma_start(out[0:P, :], windows[0][:])
        nc.vector.tensor_copy(windows[1][:].indirect(slot_sb[:]), y[1][:])
        nc.sync.dma_start(out[P:N, :], windows[1][:])
